import numpy as np
import ml_dtypes


def mxq(x, axis, fmt="e4m3"):
    dtype, down = {"e4m3": (ml_dtypes.float8_e4m3fn, 7), "e5m2": (ml_dtypes.float8_e5m2, 14)}[fmt]
    v = np.moveaxis(np.asarray(x, np.float32).astype(ml_dtypes.bfloat16).astype(np.float64), axis, -1)
    blocks = v.reshape(v.shape[:-1] + (-1, 32))
    amax = np.abs(blocks).max(-1, keepdims=True)
    byte = np.maximum(np.where(amax > 0, np.frexp(amax)[1] - 1 + 127, 0) - down, 1)
    scale = np.exp2(byte - 127.0)
    codes = (blocks / scale).astype(np.float32).astype(dtype).astype(np.float64)
    return np.moveaxis((codes * scale).reshape(v.shape), -1, axis)


WIDE = False


def mx_kscale(k):
    if not WIDE:
        return np.ones(k)
    levels = np.array([10, -10, 5, -5, 0])
    if k % 512:
        return np.exp2(np.random.permutation(np.resize(levels, k // 32))).repeat(32)
    a = np.empty((k // 512, 16))
    for p in range(k // 512):
        a[p, :8] = np.random.permutation(np.resize(levels, 8))
        for g in range(8):
            far = levels[np.abs(levels - a[p, g]) >= 10]
            a[p, g + 8] = far[np.random.randint(len(far))]
    return np.exp2(a.ravel()).repeat(32)


def f64(x):
    return np.asarray(x).astype(np.float64)


def striped(idx):
    return np.tile(idx.reshape(-1, 16).T, (8, 1)).astype(np.uint16)


def unstriped(offs):
    return offs[:16].T.reshape(-1).astype(np.int64)


E2M1 = np.array([0.0, 0.5, 1.0, 1.5, 2.0, 3.0, 4.0, 6.0, -0.0, -0.5, -1.0, -1.5, -2.0, -3.0, -4.0, -6.0])


def pack_weight(w, fmt):
    k, n = w.shape
    w = f64(np.asarray(w, np.float32).astype(ml_dtypes.bfloat16)).reshape(k // 32, 32, n)
    amax = np.abs(w).max(1)
    if fmt == "e4m3":
        byte = np.frexp(amax)[1] - 1 + 127 - 7
    else:
        mant, ex = np.frexp(amax / 6.0)
        byte = np.where(mant > 0.5, ex, ex - 1) + 127
    byte = np.clip(np.where(amax > 0, byte, 1), 1, 254)
    scaled = (w * np.exp2(127.0 - byte)[:, None, :]).reshape(k, n).astype(np.float32)
    by_word = np.ascontiguousarray(scaled.reshape(k // 512, 128, 4, n).transpose(0, 1, 3, 2))
    if fmt == "e4m3":
        words = by_word.astype(ml_dtypes.float8_e4m3fn).view(np.uint8)
    else:
        c = by_word.astype(ml_dtypes.float4_e2m1fn).view(np.uint8) & 0xF
        words = (c[..., 0::2] | (c[..., 1::2] << 4)).reshape(k // 512, 128, 2 * n)
    return np.ascontiguousarray(words), np.ascontiguousarray(byte.astype(np.uint8).reshape(k // 512, 16, n))


def unpack_weight(words, scales, fmt):
    g, _, n = scales.shape
    words = np.ascontiguousarray(words).reshape(g, 128, n, -1)
    if fmt == "e4m3":
        vals = words.view(ml_dtypes.float8_e4m3fn).astype(np.float64)
    else:
        nib = np.empty((g, 128, n, 4), np.uint8)
        nib[..., 0::2] = words & 0xF
        nib[..., 1::2] = words >> 4
        vals = E2M1[nib]
    vals = vals * np.repeat(np.exp2(scales.astype(np.float64) - 127.0), 8, axis=1)[..., None]
    return vals.transpose(0, 1, 3, 2).reshape(g * 512, n)


def gelu(v):
    return 0.5 * v * (1.0 + np.tanh(np.sqrt(2.0 / np.pi) * (v + 0.044715 * v**3)))


K, T, E, C, H, N = 1024, 640, 2, 256, 512, 512


def by_expert(wq, xq):
    return np.concatenate([wq[e].T @ xq[:, e * C:(e + 1) * C] for e in range(E)], axis=1)


def setup_inputs():
    n = np.random.standard_normal
    s = mx_kscale(K)[:, None]
    u = mx_kscale(H)
    w1 = [pack_weight(m, "e2m1") for m in n((E, K, H)) / np.sqrt(K) / s[None]]
    w3 = [pack_weight(m, "e2m1") for m in n((E, K, H)) / np.sqrt(K) / s[None] * u[None, None, :]]
    w2 = [pack_weight(m, "e2m1") for m in n((E, H, N)) / np.sqrt(H) / u[None, :, None]]
    x = pack_weight(n((K, T)) * s, "e4m3")
    return {
        "x_words": x[0],
        "x_scales": x[1],
        "w1_words": np.stack([m[0] for m in w1]),
        "w1_scales": np.stack([m[1] for m in w1]),
        "w3_words": np.stack([m[0] for m in w3]),
        "w3_scales": np.stack([m[1] for m in w3]),
        "w2_words": np.stack([m[0] for m in w2]),
        "w2_scales": np.stack([m[1] for m in w2]),
        "gate": np.tile(np.random.uniform(0.2, 1.0, E * C), (N, 1)).astype(np.float32),
        "offs": striped(np.random.permutation(T)[:E * C]),
    }


def reference(x_words, x_scales, w1_words, w1_scales, w3_words, w3_scales, w2_words, w2_scales, gate, offs):
    idx = unstriped(offs)
    w1 = np.stack([unpack_weight(w1_words[e], w1_scales[e], "e2m1") for e in range(E)])
    w3 = np.stack([unpack_weight(w3_words[e], w3_scales[e], "e2m1") for e in range(E)])
    w2 = np.stack([unpack_weight(w2_words[e], w2_scales[e], "e2m1") for e in range(E)])
    xq = unpack_weight(x_words, x_scales, "e4m3")[:, idx]
    h = gelu(by_expert(w1, xq))
    h = h * by_expert(w3, xq)
    y = by_expert(w2, mxq(h, 0, "e4m3"))
    out = np.zeros((N, T))
    out[:, idx] = f64(gate) * y
    return out

@@ -1,0 +1,171 @@
+from contextlib import ExitStack
+
+import concourse.mybir as mybir
+from concourse.masks import make_identity
+
+K, T, E, C, H, N = 1024, 640, 2, 256, 512, 512
+SLOTS = E * C
+FLOPS = 2 * SLOTS * (2 * K * H + H * N)
+
+F32 = mybir.dt.float32
+BF16 = mybir.dt.bfloat16
+I32 = mybir.dt.int32
+U32 = mybir.dt.uint32
+U16 = mybir.dt.uint16
+U8 = mybir.dt.uint8
+FP8X4 = mybir.dt.float8_e4m3fn_x4
+FP4X4 = mybir.dt.float4_e2m1fn_x4
+GELU = mybir.ActivationFunctionType.Gelu_apprx_tanh
+MULT = mybir.AluOpType.mult
+
+P = 128
+PASSES = K // 512
+BLOCK = 128
+BLOCKS = SLOTS // BLOCK
+ROWS = N // P
+SCATTERS = ((0, 1), (1, 2), (2, 3), (3, 4))
+
+
+def load_scale_rows(nc, plane, rows, groups):
+    words = rows.bitcast(I32)
+    for r in range(4):
+        nc.sync.dma_start(
+            out=plane[r:P:32, :].bitcast(I32).rearrange("p (g w) -> p g w", g=groups),
+            in_=words[:, r:16:4, :].rearrange("g q w -> q g w"),
+        )
+
+
+def tile_moe_pkd_glu_gelu_kernel(
+    tc, x_words, x_scales, w1_words, w1_scales, w3_words, w3_scales, w2_words, w2_scales, gate, offs, out
+):
+    nc = tc.nc
+    with ExitStack() as ctx:
+        held = ctx.enter_context(tc.tile_pool(name="held", bufs=1))
+        ring = ctx.enter_context(tc.tile_pool(name="ring", bufs=2))
+        picked = ctx.enter_context(tc.tile_pool(name="picked", bufs=3))
+        psum = ctx.enter_context(tc.psum_pool(name="psum", bufs=2))
+
+        offsets = held.tile([P, SLOTS // 16], U16, name="offsets")
+        nc.sync.dma_start(offsets[:], offs)
+
+        x_plane = held.tile([P, PASSES * T], U8, name="x_plane", align_bytes=64)
+        w1_plane = held.tile([P, E * PASSES * H], U8, name="w1_plane", align_bytes=64)
+        w3_plane = held.tile([P, E * PASSES * H], U8, name="w3_plane", align_bytes=64)
+        w2_plane = held.tile([P, E * N], U8, name="w2_plane", align_bytes=64)
+        for plane in (x_plane, w1_plane, w3_plane, w2_plane):
+            nc.vector.memset(plane[:].bitcast(I32), 0)
+
+        load_scale_rows(nc, x_plane, x_scales, PASSES)
+        tokens = []
+        for o in range(PASSES):
+            table = held.tile([P, T], U32, name=f"tokens{o}", align_bytes=64)
+            nc.sync.dma_start(table[:].bitcast(I32), x_words[o].rearrange("p t r -> p (t r)").bitcast(I32))
+            tokens.append(table)
+
+        def load_words(words, e, name):
+            codes = held.tile([P, PASSES, 2 * H], U8, name=name, align_bytes=64)
+            nc.sync.dma_start(codes[:].bitcast(I32), words[e].bitcast(I32).rearrange("s p w -> p s w"))
+            return codes
+
+        w1 = [load_words(w1_words, 0, "w1_0")]
+        load_scale_rows(nc, w1_plane, w1_scales.rearrange("e s q i -> (e s) q i"), E * PASSES)
+        w3 = [load_words(w3_words, 0, "w3_0")]
+        load_scale_rows(nc, w3_plane, w3_scales.rearrange("e s q i -> (e s) q i"), E * PASSES)
+        w2 = held.tile([P, E, 2 * N], U8, name="w2", align_bytes=64)
+        nc.sync.dma_start(w2[:].bitcast(I32), w2_words.bitcast(I32).rearrange("e s p w -> p (e s) w"))
+        load_scale_rows(nc, w2_plane, w2_scales.rearrange("e s q n -> (e s) q n"), E)
+        w1.append(load_words(w1_words, 1, "w1_1"))
+        w3.append(load_words(w3_words, 1, "w3_1"))
+        gates = held.tile([P, SLOTS], F32, name="gates")
+        nc.sync.dma_start(gates[:], gate[0:P, :])
+
+        zero = held.tile([P, 1], F32, name="zero")
+        nc.gpsimd.memset(zero[:], 0.0)
+        identity = held.tile([P, P], F32, name="identity")
+        make_identity(nc, identity[:])
+
+        results = []
+        for j in range(ROWS):
+            window = held.tile([P, T], F32, name=f"result{j}")
+            nc.scalar.activation(window[:], zero[:].to_broadcast([P, T]), GELU)
+            results.append(window)
+        y = held.tile([P, ROWS, SLOTS], F32, name="y")
+
+        def gather(b):
+            entries = offsets[:, b * BLOCK // 16 : (b + 1) * BLOCK // 16]
+            got = []
+            for o in range(PASSES):
+                codes = picked.tile([P, BLOCK], U32, name=f"x_codes{o}", align_bytes=64)
+                scales = picked.tile([P, BLOCK], U8, name=f"x_bytes{o}", align_bytes=64)
+                nc.vector.tensor_copy(codes[:], tokens[o][:].indirect(entries))
+                nc.vector.tensor_copy(scales[:], x_plane[:, o * T : (o + 1) * T].indirect(entries))
+                got.append((codes, scales))
+            return got
+
+        def first_layer(b, got):
+            e = b * BLOCK // C
+            sums = []
+            for name, words, plane in (("a", w1[e], w1_plane), ("b", w3[e], w3_plane)):
+                bank = psum.tile([P, H], F32, name=name)
+                for o, (codes, scales) in enumerate(got):
+                    at = (e * PASSES + o) * H
+                    nc.tensor.matmul_mx(
+                        out=bank[:],
+                        lhsT=codes[:].bitcast(FP8X4),
+                        lhsT_scale=scales[:],
+                        rhs=words[:, o, :].bitcast(FP4X4),
+                        rhs_scale=plane[:, at : at + H],
+                        start=(o == 0),
+                        stop=(o == PASSES - 1),
+                    )
+                sums.append(bank[:].rearrange("p (q u v) -> p u q v", u=2, v=2))
+            act = ring.tile([P, 2, P, 2], F32, name="act")
+            nc.scalar.activation(act[:], sums[0], GELU)
+            hidden = ring.tile([P, 2, P, 2], BF16, name="hidden", align_bytes=64)
+            nc.vector.tensor_tensor(hidden[:], sums[1], act[:], MULT)
+            return hidden
+
+        def turn(hidden):
+            pairs = hidden[:].rearrange("p u q v -> p (u q v)").bitcast(F32)
+            turned = psum.tile([P, 2, BLOCK], F32, name="turned")
+            for u in range(2):
+                nc.tensor.transpose(turned[:, u, :], pairs[:, u * P : (u + 1) * P], identity[:])
+            grouped = ring.tile([P, 4 * BLOCK], BF16, name="grouped", align_bytes=64)
+            nc.scalar.copy(
+                grouped[:].bitcast(F32).rearrange("p (r u) -> p r u", u=2), turned[:].rearrange("p u r -> p r u")
+            )
+            codes = ring.tile([P, BLOCK], U32, name="h_codes", align_bytes=64)
+            scales = ring.tile([P, BLOCK], U8, name="h_bytes", align_bytes=64)
+            nc.vector.quantize_mx(out=codes[:].bitcast(FP8X4), scales=scales[:], in_=grouped[:])
+            return codes, scales
+
+        def second_layer(b, codes, scales):
+            e = b * BLOCK // C
+            bank = psum.tile([P, ROWS, BLOCK], F32, name="y_bank")
+            for j in range(ROWS):
+                nc.tensor.matmul_mx(
+                    out=bank[:, j, :],
+                    lhsT=w2[:, e, 2 * j * P : 2 * (j + 1) * P].bitcast(FP4X4),
+                    lhsT_scale=w2_plane[:, e * N + j * P : e * N + (j + 1) * P],
+                    rhs=codes[:].bitcast(FP8X4),
+                    rhs_scale=scales[:],
+                    start=True,
+                    stop=True,
+                )
+            nc.scalar.copy(y[:, :, b * BLOCK : (b + 1) * BLOCK], bank[:])
+
+        def scatter(first, last):
+            cols = slice(first * BLOCK, last * BLOCK)
+            entries = offsets[:, first * BLOCK // 16 : last * BLOCK // 16]
+            for j in range(ROWS):
+                nc.vector.tensor_tensor(results[j][:].indirect(entries), y[:, j, cols], gates[:, cols], MULT)
+                if last == BLOCKS:
+                    nc.sync.dma_start(out[j * P : (j + 1) * P, :], results[j][:])
+
+        hidden = {0: first_layer(0, gather(0))}
+        for b in range(BLOCKS):
+            if b + 1 < BLOCKS:
+                hidden[b + 1] = first_layer(b + 1, gather(b + 1))
+            second_layer(b, *turn(hidden[b]))
+        for first, last in SCATTERS:
+            scatter(first, last)

@@ -23,7 +23,8 @@ PASSES = K // 512
 BLOCK = 128
 BLOCKS = SLOTS // BLOCK
 ROWS = N // P
-SCATTERS = ((0, 1), (1, 2), (2, 3), (3, 4))
+HALVES = C // BLOCK
+WINDOW = 704
 
 
 def load_scale_rows(nc, plane, rows, groups):
@@ -42,8 +43,7 @@ def tile_moe_pkd_glu_gelu_kernel(
     with ExitStack() as ctx:
         held = ctx.enter_context(tc.tile_pool(name="held", bufs=1))
         ring = ctx.enter_context(tc.tile_pool(name="ring", bufs=2))
-        picked = ctx.enter_context(tc.tile_pool(name="picked", bufs=3))
-        psum = ctx.enter_context(tc.psum_pool(name="psum", bufs=2))
+        psum = ctx.enter_context(tc.psum_pool(name="psum", bufs=1))
 
         offsets = held.tile([P, SLOTS // 16], U16, name="offsets")
         nc.sync.dma_start(offsets[:], offs)
@@ -55,12 +55,15 @@ def tile_moe_pkd_glu_gelu_kernel(
         for plane in (x_plane, w1_plane, w3_plane, w2_plane):
             nc.vector.memset(plane[:].bitcast(I32), 0)
 
+        def load_tokens(o, columns):
+            table = held.tile([P, columns], U32, name=f"tokens{o}", tag=f"pass{o}", align_bytes=64)
+            nc.sync.dma_start(table[:, 0:T].bitcast(I32), x_words[o].rearrange("p t r -> p (t r)").bitcast(I32))
+            return table
+
+        tokens = [load_tokens(0, WINDOW)]
+        nc.gpsimd.memset(tokens[0][:, T:WINDOW].bitcast(I32), 0)
         load_scale_rows(nc, x_plane, x_scales, PASSES)
-        tokens = []
-        for o in range(PASSES):
-            table = held.tile([P, T], U32, name=f"tokens{o}", align_bytes=64)
-            nc.sync.dma_start(table[:].bitcast(I32), x_words[o].rearrange("p t r -> p (t r)").bitcast(I32))
-            tokens.append(table)
+        tokens.append(load_tokens(1, T))
 
         def load_words(words, e, name):
             codes = held.tile([P, PASSES, 2 * H], U8, name=name, align_bytes=64)
@@ -71,11 +74,11 @@ def tile_moe_pkd_glu_gelu_kernel(
         load_scale_rows(nc, w1_plane, w1_scales.rearrange("e s q i -> (e s) q i"), E * PASSES)
         w3 = [load_words(w3_words, 0, "w3_0")]
         load_scale_rows(nc, w3_plane, w3_scales.rearrange("e s q i -> (e s) q i"), E * PASSES)
+        w1.append(load_words(w1_words, 1, "w1_1"))
+        w3.append(load_words(w3_words, 1, "w3_1"))
         w2 = held.tile([P, E, 2 * N], U8, name="w2", align_bytes=64)
         nc.sync.dma_start(w2[:].bitcast(I32), w2_words.bitcast(I32).rearrange("e s p w -> p (e s) w"))
         load_scale_rows(nc, w2_plane, w2_scales.rearrange("e s q n -> (e s) q n"), E)
-        w1.append(load_words(w1_words, 1, "w1_1"))
-        w3.append(load_words(w3_words, 1, "w3_1"))
         gates = held.tile([P, SLOTS], F32, name="gates")
         nc.sync.dma_start(gates[:], gate[0:P, :])
 
@@ -91,60 +94,81 @@ def tile_moe_pkd_glu_gelu_kernel(
             results.append(window)
         y = held.tile([P, ROWS, SLOTS], F32, name="y")
 
-        def gather(b):
-            entries = offsets[:, b * BLOCK // 16 : (b + 1) * BLOCK // 16]
-            got = []
+        def entries_of(e):
+            return offsets[:, e * C // 16 : (e + 1) * C // 16]
+
+        x_codes = [held.tile([P, SLOTS], U32, name=f"x_codes{o}", align_bytes=64) for o in range(PASSES)]
+        x_bytes = []
+
+        def gather_bytes(e):
+            scales = held.tile([P, PASSES, C], U8, name=f"x_bytes{e}", tag=f"pass{e}", align_bytes=64)
             for o in range(PASSES):
-                codes = picked.tile([P, BLOCK], U32, name=f"x_codes{o}", align_bytes=64)
-                scales = picked.tile([P, BLOCK], U8, name=f"x_bytes{o}", align_bytes=64)
-                nc.vector.tensor_copy(codes[:], tokens[o][:].indirect(entries))
-                nc.vector.tensor_copy(scales[:], x_plane[:, o * T : (o + 1) * T].indirect(entries))
-                got.append((codes, scales))
-            return got
+                nc.vector.tensor_copy(scales[:, o, :], x_plane[:, o * T : (o + 1) * T].indirect(entries_of(e)))
+            x_bytes.append(scales)
 
-        def first_layer(b, got):
-            e = b * BLOCK // C
-            sums = []
-            for name, words, plane in (("a", w1[e], w1_plane), ("b", w3[e], w3_plane)):
-                bank = psum.tile([P, H], F32, name=name)
-                for o, (codes, scales) in enumerate(got):
-                    at = (e * PASSES + o) * H
-                    nc.tensor.matmul_mx(
-                        out=bank[:],
-                        lhsT=codes[:].bitcast(FP8X4),
-                        lhsT_scale=scales[:],
-                        rhs=words[:, o, :].bitcast(FP4X4),
-                        rhs_scale=plane[:, at : at + H],
-                        start=(o == 0),
-                        stop=(o == PASSES - 1),
-                    )
-                sums.append(bank[:].rearrange("p (q u v) -> p u q v", u=2, v=2))
+        nc.vector.tensor_copy(x_codes[0][:], tokens[0][:].indirect(offsets[:]))
+        gather_bytes(0)
+        for e in range(E):
+            nc.vector.tensor_copy(x_codes[1][:, e * C : (e + 1) * C], tokens[1][:].indirect(entries_of(e)))
+        gather_bytes(1)
+
+        def multiply(bank, e, half, o, words, plane):
+            cols = slice(e * C + half * BLOCK, e * C + (half + 1) * BLOCK)
+            at = (e * PASSES + o) * H
+            nc.tensor.matmul_mx(
+                out=bank[:],
+                lhsT=x_codes[o][:, cols].bitcast(FP8X4),
+                lhsT_scale=x_bytes[e][:, o, half * BLOCK : (half + 1) * BLOCK],
+                rhs=words[:, o, :].bitcast(FP4X4),
+                rhs_scale=plane[:, at : at + H],
+                start=(o == 0),
+                stop=(o == PASSES - 1),
+            )
+
+        def by_pairs(bank):
+            return bank[:].rearrange("p (q u v) -> p u q v", u=2, v=2)
+
+        def open_gate(e, half, bank):
+            a = psum.tile([P, H], F32, name=f"a{e}{half}", tag=bank)
+            multiply(a, e, half, 0, w1[e], w1_plane)
+            return a
+
+        def close_gate(e, half, a):
+            multiply(a, e, half, 1, w1[e], w1_plane)
             act = ring.tile([P, 2, P, 2], F32, name="act")
-            nc.scalar.activation(act[:], sums[0], GELU)
-            hidden = ring.tile([P, 2, P, 2], BF16, name="hidden", align_bytes=64)
-            nc.vector.tensor_tensor(hidden[:], sums[1], act[:], MULT)
-            return hidden
+            nc.scalar.activation(act[:], by_pairs(a), GELU)
+            return act
 
-        def turn(hidden):
+        def hidden_values(e, half, act, bank):
+            b = psum.tile([P, H], F32, name=f"b{e}{half}", tag=bank)
+            for o in range(PASSES):
+                multiply(b, e, half, o, w3[e], w3_plane)
+            product = ring.tile([P, 2, P, 2], BF16, name="hidden", align_bytes=64)
+            nc.vector.tensor_tensor(product[:], by_pairs(b), act[:], MULT)
+            return product
+
+        def turn(hidden, grouped, half, bank):
             pairs = hidden[:].rearrange("p u q v -> p (u q v)").bitcast(F32)
-            turned = psum.tile([P, 2, BLOCK], F32, name="turned")
+            turned = psum.tile([P, 2, BLOCK], F32, name="turned", tag=bank)
             for u in range(2):
                 nc.tensor.transpose(turned[:, u, :], pairs[:, u * P : (u + 1) * P], identity[:])
-            grouped = ring.tile([P, 4 * BLOCK], BF16, name="grouped", align_bytes=64)
             nc.scalar.copy(
-                grouped[:].bitcast(F32).rearrange("p (r u) -> p r u", u=2), turned[:].rearrange("p u r -> p r u")
+                grouped[:, 4 * half * BLOCK : 4 * (half + 1) * BLOCK].bitcast(F32).rearrange("p (r u) -> p r u", u=2),
+                turned[:].rearrange("p u r -> p r u"),
             )
-            codes = ring.tile([P, BLOCK], U32, name="h_codes", align_bytes=64)
-            scales = ring.tile([P, BLOCK], U8, name="h_bytes", align_bytes=64)
+
+        def quantise(grouped):
+            codes = ring.tile([P, C], U32, name="h_codes", align_bytes=64)
+            scales = ring.tile([P, C], U8, name="h_bytes", align_bytes=64)
             nc.vector.quantize_mx(out=codes[:].bitcast(FP8X4), scales=scales[:], in_=grouped[:])
             return codes, scales
 
-        def second_layer(b, codes, scales):
-            e = b * BLOCK // C
-            bank = psum.tile([P, ROWS, BLOCK], F32, name="y_bank")
-            for j in range(ROWS):
+        def second_layer(e, rows, quantised, bank):
+            codes, scales = quantised
+            sums = psum.tile([P, len(rows), C], F32, name="y_bank", tag=bank)
+            for j in rows:
                 nc.tensor.matmul_mx(
-                    out=bank[:, j, :],
+                    out=sums[:, j - rows[0], :],
                     lhsT=w2[:, e, 2 * j * P : 2 * (j + 1) * P].bitcast(FP4X4),
                     lhsT_scale=w2_plane[:, e * N + j * P : e * N + (j + 1) * P],
                     rhs=codes[:].bitcast(FP8X4),
@@ -152,20 +176,35 @@ def tile_moe_pkd_glu_gelu_kernel(
                     start=True,
                     stop=True,
                 )
-            nc.scalar.copy(y[:, :, b * BLOCK : (b + 1) * BLOCK], bank[:])
+            nc.scalar.copy(y[:, rows[0] : rows[-1] + 1, e * C : (e + 1) * C], sums[:])
 
-        def scatter(first, last):
-            cols = slice(first * BLOCK, last * BLOCK)
-            entries = offsets[:, first * BLOCK // 16 : last * BLOCK // 16]
+        def scatter(e):
+            cols = slice(e * C, (e + 1) * C)
             for j in range(ROWS):
-                nc.vector.tensor_tensor(results[j][:].indirect(entries), y[:, j, cols], gates[:, cols], MULT)
-                if last == BLOCKS:
+                nc.vector.tensor_tensor(results[j][:].indirect(entries_of(e)), y[:, j, cols], gates[:, cols], MULT)
+                if e == E - 1:
                     nc.sync.dma_start(out[j * P : (j + 1) * P, :], results[j][:])
 
-        hidden = {0: first_layer(0, gather(0))}
-        for b in range(BLOCKS):
-            if b + 1 < BLOCKS:
-                hidden[b + 1] = first_layer(b + 1, gather(b + 1))
-            second_layer(b, *turn(hidden[b]))
-        for first, last in SCATTERS:
-            scatter(first, last)
+        grouped = [ring.tile([P, 4 * C], BF16, name="grouped", align_bytes=64) for e in range(E)]
+
+        a = [open_gate(0, half, f"bank{half}") for half in range(HALVES)]
+        acts = [close_gate(0, half, a[half]) for half in range(HALVES)]
+        hidden = [hidden_values(0, half, acts[half], f"bank{2 + half}") for half in range(HALVES)]
+        for half in range(HALVES):
+            turn(hidden[half], grouped[0], half, f"bank{4 + half}")
+        first = quantise(grouped[0])
+        second_layer(0, (0,), first, "bank6")
+
+        hidden = [
+            hidden_values(1, 0, close_gate(1, 0, open_gate(1, 0, "bank7")), "bank0"),
+            hidden_values(1, 1, close_gate(1, 1, open_gate(1, 1, "bank1")), "bank2"),
+        ]
+        second_layer(0, (1,), first, "bank1")
+        for half in range(HALVES):
+            turn(hidden[half], grouped[1], half, f"bank{4 + half}")
+        second = quantise(grouped[1])
+        second_layer(0, (2, 3), first, "bank5")
+        second_layer(1, (0, 1), second, "bank3")
+        second_layer(1, (2, 3), second, "bank7")
+        for e in range(E):
+            scatter(e)

@@ -46,7 +46,6 @@ def tile_moe_pkd_glu_gelu_kernel(
         psum = ctx.enter_context(tc.psum_pool(name="psum", bufs=1))
 
         offsets = held.tile([P, SLOTS // 16], U16, name="offsets")
-        nc.sync.dma_start(offsets[:], offs)
 
         x_plane = held.tile([P, PASSES * T], U8, name="x_plane", align_bytes=64)
         w1_plane = held.tile([P, E * PASSES * H], U8, name="w1_plane", align_bytes=64)
@@ -60,25 +59,25 @@ def tile_moe_pkd_glu_gelu_kernel(
             nc.sync.dma_start(table[:, 0:T].bitcast(I32), x_words[o].rearrange("p t r -> p (t r)").bitcast(I32))
             return table
 
-        tokens = [load_tokens(0, WINDOW)]
-        nc.gpsimd.memset(tokens[0][:, T:WINDOW].bitcast(I32), 0)
-        load_scale_rows(nc, x_plane, x_scales, PASSES)
-        tokens.append(load_tokens(1, T))
-
         def load_words(words, e, name):
             codes = held.tile([P, PASSES, 2 * H], U8, name=name, align_bytes=64)
             nc.sync.dma_start(codes[:].bitcast(I32), words[e].bitcast(I32).rearrange("s p w -> p s w"))
             return codes
 
+        nc.sync.dma_start(offsets[:], offs)
+        tokens = [load_tokens(0, WINDOW)]
+        nc.gpsimd.memset(tokens[0][:, T:WINDOW].bitcast(I32), 0)
+        load_scale_rows(nc, x_plane, x_scales, PASSES)
+        tokens.append(load_tokens(1, T))
         w1 = [load_words(w1_words, 0, "w1_0")]
         load_scale_rows(nc, w1_plane, w1_scales.rearrange("e s q i -> (e s) q i"), E * PASSES)
         w3 = [load_words(w3_words, 0, "w3_0")]
         load_scale_rows(nc, w3_plane, w3_scales.rearrange("e s q i -> (e s) q i"), E * PASSES)
-        w1.append(load_words(w1_words, 1, "w1_1"))
-        w3.append(load_words(w3_words, 1, "w3_1"))
         w2 = held.tile([P, E, 2 * N], U8, name="w2", align_bytes=64)
         nc.sync.dma_start(w2[:].bitcast(I32), w2_words.bitcast(I32).rearrange("e s p w -> p (e s) w"))
+        w1.append(load_words(w1_words, 1, "w1_1"))
         load_scale_rows(nc, w2_plane, w2_scales.rearrange("e s q n -> (e s) q n"), E)
+        w3.append(load_words(w3_words, 1, "w3_1"))
         gates = held.tile([P, SLOTS], F32, name="gates")
         nc.sync.dma_start(gates[:], gate[0:P, :])
 
@@ -157,33 +156,35 @@ def tile_moe_pkd_glu_gelu_kernel(
                 turned[:].rearrange("p u r -> p r u"),
             )
 
-        def quantise(grouped):
-            codes = ring.tile([P, C], U32, name="h_codes", align_bytes=64)
-            scales = ring.tile([P, C], U8, name="h_bytes", align_bytes=64)
-            nc.vector.quantize_mx(out=codes[:].bitcast(FP8X4), scales=scales[:], in_=grouped[:])
-            return codes, scales
+        h_codes = [held.tile([P, C], U32, name=f"h_codes{e}", align_bytes=64) for e in range(E)]
+        h_bytes = [held.tile([P, C], U8, name=f"h_bytes{e}", align_bytes=64) for e in range(E)]
 
-        def second_layer(e, rows, quantised, bank):
-            codes, scales = quantised
-            sums = psum.tile([P, len(rows), C], F32, name="y_bank", tag=bank)
+        def quantise(e, first, count):
+            nc.vector.quantize_mx(
+                out=h_codes[e][:, first : first + count].bitcast(FP8X4),
+                scales=h_bytes[e][:, first : first + count],
+                in_=grouped[e][:, 4 * first : 4 * (first + count)],
+            )
+
+        def second_layer(e, first, count, rows, bank):
+            sums = psum.tile([P, len(rows), count], F32, name="y_bank", tag=bank)
             for j in rows:
                 nc.tensor.matmul_mx(
                     out=sums[:, j - rows[0], :],
                     lhsT=w2[:, e, 2 * j * P : 2 * (j + 1) * P].bitcast(FP4X4),
                     lhsT_scale=w2_plane[:, e * N + j * P : e * N + (j + 1) * P],
-                    rhs=codes[:].bitcast(FP8X4),
-                    rhs_scale=scales[:],
+                    rhs=h_codes[e][:, first : first + count].bitcast(FP8X4),
+                    rhs_scale=h_bytes[e][:, first : first + count],
                     start=True,
                     stop=True,
                 )
-            nc.scalar.copy(y[:, rows[0] : rows[-1] + 1, e * C : (e + 1) * C], sums[:])
+            slot = e * C + first
+            nc.scalar.copy(y[:, rows[0] : rows[-1] + 1, slot : slot + count], sums[:])
 
-        def scatter(e):
-            cols = slice(e * C, (e + 1) * C)
-            for j in range(ROWS):
-                nc.vector.tensor_tensor(results[j][:].indirect(entries_of(e)), y[:, j, cols], gates[:, cols], MULT)
-                if e == E - 1:
-                    nc.sync.dma_start(out[j * P : (j + 1) * P, :], results[j][:])
+        def scatter(j, slot, count):
+            cols = slice(slot, slot + count)
+            entries = offsets[:, slot // 16 : (slot + count) // 16]
+            nc.vector.tensor_tensor(results[j][:].indirect(entries), y[:, j, cols], gates[:, cols], MULT)
 
         grouped = [ring.tile([P, 4 * C], BF16, name="grouped", align_bytes=64) for e in range(E)]
 
@@ -192,19 +193,24 @@ def tile_moe_pkd_glu_gelu_kernel(
         hidden = [hidden_values(0, half, acts[half], f"bank{2 + half}") for half in range(HALVES)]
         for half in range(HALVES):
             turn(hidden[half], grouped[0], half, f"bank{4 + half}")
-        first = quantise(grouped[0])
-        second_layer(0, (0,), first, "bank6")
+            quantise(0, half * BLOCK, BLOCK)
 
-        hidden = [
-            hidden_values(1, 0, close_gate(1, 0, open_gate(1, 0, "bank7")), "bank0"),
-            hidden_values(1, 1, close_gate(1, 1, open_gate(1, 1, "bank1")), "bank2"),
-        ]
-        second_layer(0, (1,), first, "bank1")
+        hidden = []
         for half in range(HALVES):
-            turn(hidden[half], grouped[1], half, f"bank{4 + half}")
-        second = quantise(grouped[1])
-        second_layer(0, (2, 3), first, "bank5")
-        second_layer(1, (0, 1), second, "bank3")
-        second_layer(1, (2, 3), second, "bank7")
-        for e in range(E):
-            scatter(e)
+            act = close_gate(1, half, open_gate(1, half, f"bank{6 + half}"))
+            second_layer(0, half * BLOCK, BLOCK, (0,), f"bank{6 + half}")
+            hidden.append(hidden_values(1, half, act, f"bank{4 + half}"))
+        second_layer(0, 0, C, (1,), "bank4")
+        for half in range(HALVES):
+            turn(hidden[half], grouped[1], half, f"bank{half}")
+        quantise(1, 0, C)
+        second_layer(0, 0, C, (2, 3), "bank1")
+        second_layer(1, 0, C, (0, 1), "bank2")
+        second_layer(1, 0, C, (2, 3), "bank3")
+        for half in range(HALVES):
+            scatter(0, half * BLOCK, BLOCK)
+        for j in range(1, ROWS):
+            scatter(j, 0, C)
+        for j in range(ROWS):
+            scatter(j, C, C)
+            nc.sync.dma_start(out[j * P : (j + 1) * P, :], results[j][:])

@@ -25,6 +25,7 @@ BLOCKS = SLOTS // BLOCK
 ROWS = N // P
 HALVES = C // BLOCK
 WINDOW = 704
+WARM_UP = 11
 
 
 def load_scale_rows(nc, plane, rows, groups):
@@ -68,8 +69,8 @@ def tile_moe_pkd_glu_gelu_kernel(
         tokens = [load_tokens(0, WINDOW)]
         nc.gpsimd.memset(tokens[0][:, T:WINDOW].bitcast(I32), 0)
         load_scale_rows(nc, x_plane, x_scales, PASSES)
-        tokens.append(load_tokens(1, T))
         w1 = [load_words(w1_words, 0, "w1_0")]
+        tokens.append(load_tokens(1, T))
         load_scale_rows(nc, w1_plane, w1_scales.rearrange("e s q i -> (e s) q i"), E * PASSES)
         w3 = [load_words(w3_words, 0, "w3_0")]
         load_scale_rows(nc, w3_plane, w3_scales.rearrange("e s q i -> (e s) q i"), E * PASSES)
@@ -92,6 +93,23 @@ def tile_moe_pkd_glu_gelu_kernel(
             nc.scalar.activation(window[:], zero[:].to_broadcast([P, T]), GELU)
             results.append(window)
         y = held.tile([P, ROWS, SLOTS], F32, name="y")
+
+        nothing = held.tile([P, 4 * BLOCK], BF16, name="nothing", align_bytes=64)
+        nc.vector.memset(nothing[:].bitcast(I32), 0)
+        idle_codes = held.tile([P, BLOCK], U32, name="idle_codes", align_bytes=64)
+        idle_bytes = held.tile([P, BLOCK], U8, name="idle_bytes", align_bytes=64)
+        nc.vector.quantize_mx(out=idle_codes[:].bitcast(FP8X4), scales=idle_bytes[:], in_=nothing[:])
+        unread = psum.tile([P, BLOCK], F32, name="unread", tag="bank6")
+        for repeat in range(WARM_UP):
+            nc.tensor.matmul_mx(
+                out=unread[:],
+                lhsT=w1[0][:, 0, 0 : 2 * P].bitcast(FP4X4),
+                lhsT_scale=idle_bytes[:],
+                rhs=idle_codes[:].bitcast(FP8X4),
+                rhs_scale=idle_bytes[:],
+                start=True,
+                stop=True,
+            )
 
         def entries_of(e):
             return offsets[:, e * C // 16 : (e + 1) * C // 16]

@@ -25,13 +25,15 @@ BLOCKS = SLOTS // BLOCK
 ROWS = N // P
 HALVES = C // BLOCK
 WINDOW = 704
-WARM_UP = 11
+GATE_BANKS = ("bank0", "bank2", "bank4", "bank0")
+UP_BANKS = ("bank1", "bank3", "bank5", "bank5")
+TURN_BANKS = ("bank1", "bank3", "bank7", "bank5")
 
 
-def load_scale_rows(nc, plane, rows, groups):
+def load_scale_rows(queues, plane, rows, groups, which=range(4)):
     words = rows.bitcast(I32)
-    for r in range(4):
-        nc.sync.dma_start(
+    for r in which:
+        queues[r % len(queues)].dma_start(
             out=plane[r:P:32, :].bitcast(I32).rearrange("p (g w) -> p g w", g=groups),
             in_=words[:, r:16:4, :].rearrange("g q w -> q g w"),
         )
@@ -43,7 +45,6 @@ def tile_moe_pkd_glu_gelu_kernel(
     nc = tc.nc
     with ExitStack() as ctx:
         held = ctx.enter_context(tc.tile_pool(name="held", bufs=1))
-        ring = ctx.enter_context(tc.tile_pool(name="ring", bufs=2))
         psum = ctx.enter_context(tc.psum_pool(name="psum", bufs=1))
 
         offsets = held.tile([P, SLOTS // 16], U16, name="offsets")
@@ -52,11 +53,17 @@ def tile_moe_pkd_glu_gelu_kernel(
         w1_plane = held.tile([P, E * PASSES * H], U8, name="w1_plane", align_bytes=64)
         w3_plane = held.tile([P, E * PASSES * H], U8, name="w3_plane", align_bytes=64)
         w2_plane = held.tile([P, E * N], U8, name="w2_plane", align_bytes=64)
-        for plane in (x_plane, w1_plane, w3_plane, w2_plane):
+        nc.gpsimd.memset(x_plane[:].bitcast(I32), 0)
+        for plane in (w1_plane, w3_plane):
             nc.vector.memset(plane[:].bitcast(I32), 0)
+        nothing = held.tile([P, 4 * H], BF16, name="nothing", align_bytes=64)
+        nc.gpsimd.memset(nothing[:].bitcast(I32), 0)
+        identity = held.tile([P, P], F32, name="identity")
+        make_identity(nc, identity[:])
+        nc.gpsimd.memset(w2_plane[:].bitcast(I32), 0)
 
         def load_tokens(o, columns):
-            table = held.tile([P, columns], U32, name=f"tokens{o}", tag=f"pass{o}", align_bytes=64)
+            table = held.tile([P, columns], U32, name=f"tokens{o}", tag=f"tokens{o}", align_bytes=64)
             nc.sync.dma_start(table[:, 0:T].bitcast(I32), x_words[o].rearrange("p t r -> p (t r)").bitcast(I32))
             return table
 
@@ -65,27 +72,27 @@ def tile_moe_pkd_glu_gelu_kernel(
             nc.sync.dma_start(codes[:].bitcast(I32), words[e].bitcast(I32).rearrange("s p w -> p s w"))
             return codes
 
-        nc.sync.dma_start(offsets[:], offs)
         tokens = [load_tokens(0, WINDOW)]
-        nc.gpsimd.memset(tokens[0][:, T:WINDOW].bitcast(I32), 0)
-        load_scale_rows(nc, x_plane, x_scales, PASSES)
-        w1 = [load_words(w1_words, 0, "w1_0")]
+        nc.vector.memset(tokens[0][:, T:WINDOW].bitcast(I32), 0)
+        nc.sync.dma_start(offsets[:], offs)
+        load_scale_rows((nc.scalar, nc.sync), x_plane, x_scales, PASSES)
         tokens.append(load_tokens(1, T))
-        load_scale_rows(nc, w1_plane, w1_scales.rearrange("e s q i -> (e s) q i"), E * PASSES)
+        w1_rows = w1_scales.rearrange("e s q i -> (e s) q i")
+        load_scale_rows((nc.sync,), w1_plane, w1_rows, E * PASSES, (0, 1))
+        w1 = [load_words(w1_words, 0, "w1_0")]
+        load_scale_rows((nc.sync,), w1_plane, w1_rows, E * PASSES, (2, 3))
         w3 = [load_words(w3_words, 0, "w3_0")]
-        load_scale_rows(nc, w3_plane, w3_scales.rearrange("e s q i -> (e s) q i"), E * PASSES)
+        load_scale_rows((nc.sync,), w3_plane, w3_scales.rearrange("e s q i -> (e s) q i"), E * PASSES)
+        w1.append(load_words(w1_words, 1, "w1_1"))
+        load_scale_rows((nc.sync,), w2_plane, w2_scales.rearrange("e s q n -> (e s) q n"), E)
+        w3.append(load_words(w3_words, 1, "w3_1"))
         w2 = held.tile([P, E, 2 * N], U8, name="w2", align_bytes=64)
         nc.sync.dma_start(w2[:].bitcast(I32), w2_words.bitcast(I32).rearrange("e s p w -> p (e s) w"))
-        w1.append(load_words(w1_words, 1, "w1_1"))
-        load_scale_rows(nc, w2_plane, w2_scales.rearrange("e s q n -> (e s) q n"), E)
-        w3.append(load_words(w3_words, 1, "w3_1"))
         gates = held.tile([P, SLOTS], F32, name="gates")
         nc.sync.dma_start(gates[:], gate[0:P, :])
 
         zero = held.tile([P, 1], F32, name="zero")
-        nc.gpsimd.memset(zero[:], 0.0)
-        identity = held.tile([P, P], F32, name="identity")
-        make_identity(nc, identity[:])
+        nc.vector.memset(zero[:], 0.0)
 
         results = []
         for j in range(ROWS):
@@ -94,83 +101,61 @@ def tile_moe_pkd_glu_gelu_kernel(
             results.append(window)
         y = held.tile([P, ROWS, SLOTS], F32, name="y")
 
-        nothing = held.tile([P, 4 * BLOCK], BF16, name="nothing", align_bytes=64)
-        nc.vector.memset(nothing[:].bitcast(I32), 0)
-        idle_codes = held.tile([P, BLOCK], U32, name="idle_codes", align_bytes=64)
-        idle_bytes = held.tile([P, BLOCK], U8, name="idle_bytes", align_bytes=64)
-        nc.vector.quantize_mx(out=idle_codes[:].bitcast(FP8X4), scales=idle_bytes[:], in_=nothing[:])
-        unread = psum.tile([P, BLOCK], F32, name="unread", tag="bank6")
-        for repeat in range(WARM_UP):
-            nc.tensor.matmul_mx(
-                out=unread[:],
-                lhsT=w1[0][:, 0, 0 : 2 * P].bitcast(FP4X4),
-                lhsT_scale=idle_bytes[:],
-                rhs=idle_codes[:].bitcast(FP8X4),
-                rhs_scale=idle_bytes[:],
-                start=True,
-                stop=True,
-            )
-
         def entries_of(e):
             return offsets[:, e * C // 16 : (e + 1) * C // 16]
 
         x_codes = [held.tile([P, SLOTS], U32, name=f"x_codes{o}", align_bytes=64) for o in range(PASSES)]
         x_bytes = []
 
-        def gather_bytes(e):
-            scales = held.tile([P, PASSES, C], U8, name=f"x_bytes{e}", tag=f"pass{e}", align_bytes=64)
+        def gather_bytes(e, tag):
+            scales = held.tile([P, PASSES, C], U8, name=f"x_bytes{e}", tag=tag, align_bytes=64)
             for o in range(PASSES):
                 nc.vector.tensor_copy(scales[:, o, :], x_plane[:, o * T : (o + 1) * T].indirect(entries_of(e)))
             x_bytes.append(scales)
 
-        nc.vector.tensor_copy(x_codes[0][:], tokens[0][:].indirect(offsets[:]))
-        gather_bytes(0)
-        for e in range(E):
-            nc.vector.tensor_copy(x_codes[1][:, e * C : (e + 1) * C], tokens[1][:].indirect(entries_of(e)))
-        gather_bytes(1)
-
-        def multiply(bank, e, half, o, words, plane):
-            cols = slice(e * C + half * BLOCK, e * C + (half + 1) * BLOCK)
+        def multiply(sums, block, o, words, plane):
+            e, half = divmod(block, HALVES)
             at = (e * PASSES + o) * H
             nc.tensor.matmul_mx(
-                out=bank[:],
-                lhsT=x_codes[o][:, cols].bitcast(FP8X4),
+                out=sums[:],
+                lhsT=x_codes[o][:, block * BLOCK : (block + 1) * BLOCK].bitcast(FP8X4),
                 lhsT_scale=x_bytes[e][:, o, half * BLOCK : (half + 1) * BLOCK],
-                rhs=words[:, o, :].bitcast(FP4X4),
+                rhs=words[e][:, o, :].bitcast(FP4X4),
                 rhs_scale=plane[:, at : at + H],
                 start=(o == 0),
                 stop=(o == PASSES - 1),
             )
 
+        def gate_sums(blocks):
+            banks = [psum.tile([P, H], F32, name=f"a{block}", tag=GATE_BANKS[block]) for block in blocks]
+            for o in range(PASSES):
+                for block, sums in zip(blocks, banks):
+                    multiply(sums, block, o, w1, w1_plane)
+            return banks
+
         def by_pairs(bank):
             return bank[:].rearrange("p (q u v) -> p u q v", u=2, v=2)
 
-        def open_gate(e, half, bank):
-            a = psum.tile([P, H], F32, name=f"a{e}{half}", tag=bank)
-            multiply(a, e, half, 0, w1[e], w1_plane)
-            return a
-
-        def close_gate(e, half, a):
-            multiply(a, e, half, 1, w1[e], w1_plane)
-            act = ring.tile([P, 2, P, 2], F32, name="act")
+        def hidden_values(block, a):
+            act = held.tile([P, 2, P, 2], F32, name=f"act{block}", align_bytes=64)
             nc.scalar.activation(act[:], by_pairs(a), GELU)
-            return act
-
-        def hidden_values(e, half, act, bank):
-            b = psum.tile([P, H], F32, name=f"b{e}{half}", tag=bank)
+            b = psum.tile([P, H], F32, name=f"b{block}", tag=UP_BANKS[block])
             for o in range(PASSES):
-                multiply(b, e, half, o, w3[e], w3_plane)
-            product = ring.tile([P, 2, P, 2], BF16, name="hidden", align_bytes=64)
+                multiply(b, block, o, w3, w3_plane)
+            product = held.tile([P, 2, P, 2], BF16, name=f"hidden{block}", align_bytes=64)
             nc.vector.tensor_tensor(product[:], by_pairs(b), act[:], MULT)
             return product
 
-        def turn(hidden, grouped, half, bank):
+        grouped = [held.tile([P, 4 * C], BF16, name=f"grouped{e}", align_bytes=64) for e in range(E)]
+
+        def turn(block, hidden):
+            e, half = divmod(block, HALVES)
             pairs = hidden[:].rearrange("p u q v -> p (u q v)").bitcast(F32)
-            turned = psum.tile([P, 2, BLOCK], F32, name="turned", tag=bank)
+            turned = psum.tile([P, 2, BLOCK], F32, name=f"turned{block}", tag=TURN_BANKS[block])
             for u in range(2):
                 nc.tensor.transpose(turned[:, u, :], pairs[:, u * P : (u + 1) * P], identity[:])
             nc.scalar.copy(
-                grouped[:, 4 * half * BLOCK : 4 * (half + 1) * BLOCK].bitcast(F32).rearrange("p (r u) -> p r u", u=2),
+                grouped[e][:, 4 * half * BLOCK : 4 * (half + 1) * BLOCK].bitcast(F32).rearrange("p (r u) -> p r u", u=2),
                 turned[:].rearrange("p u r -> p r u"),
             )
 
@@ -204,26 +189,46 @@ def tile_moe_pkd_glu_gelu_kernel(
             entries = offsets[:, slot // 16 : (slot + count) // 16]
             nc.vector.tensor_tensor(results[j][:].indirect(entries), y[:, j, cols], gates[:, cols], MULT)
 
-        grouped = [ring.tile([P, 4 * C], BF16, name="grouped", align_bytes=64) for e in range(E)]
+        idle_codes = held.tile([P, H], U32, name="idle_codes", align_bytes=64)
+        idle_bytes = held.tile([P, H], U8, name="idle_bytes", align_bytes=64)
+        nc.vector.quantize_mx(out=idle_codes[:].bitcast(FP8X4), scales=idle_bytes[:], in_=nothing[:])
+        unread = psum.tile([P, H], F32, name="unread", tag="bank6")
 
-        a = [open_gate(0, half, f"bank{half}") for half in range(HALVES)]
-        acts = [close_gate(0, half, a[half]) for half in range(HALVES)]
-        hidden = [hidden_values(0, half, acts[half], f"bank{2 + half}") for half in range(HALVES)]
+        def warm_up(codes):
+            for repeat in range(2):
+                nc.tensor.matmul_mx(
+                    out=unread[:],
+                    lhsT=codes[:, 0:P].bitcast(FP8X4),
+                    lhsT_scale=idle_bytes[:, 0:P],
+                    rhs=idle_codes[:, 0 : H // 2].bitcast(U8).bitcast(FP4X4),
+                    rhs_scale=idle_bytes[:],
+                    start=True,
+                    stop=True,
+                )
+
+        warm_up(idle_codes)
+        nc.vector.tensor_copy(x_codes[0][:], tokens[0][:].indirect(offsets[:]))
+        warm_up(x_codes[0])
+        gather_bytes(0, "x_bytes0")
+        for e in range(E):
+            nc.vector.tensor_copy(x_codes[1][:, e * C : (e + 1) * C], tokens[1][:].indirect(entries_of(e)))
+        gather_bytes(1, "tokens1")
+
+        hidden = [hidden_values(block, a) for block, a in enumerate(gate_sums((0, 1)))]
         for half in range(HALVES):
-            turn(hidden[half], grouped[0], half, f"bank{4 + half}")
+            turn(half, hidden[half])
             quantise(0, half * BLOCK, BLOCK)
-
-        hidden = []
-        for half in range(HALVES):
-            act = close_gate(1, half, open_gate(1, half, f"bank{6 + half}"))
-            second_layer(0, half * BLOCK, BLOCK, (0,), f"bank{6 + half}")
-            hidden.append(hidden_values(1, half, act, f"bank{4 + half}"))
-        second_layer(0, 0, C, (1,), "bank4")
-        for half in range(HALVES):
-            turn(hidden[half], grouped[1], half, f"bank{half}")
+        hidden.append(hidden_values(2, gate_sums((2,))[0]))
+        second_layer(0, 0, BLOCK, (0,), "bank0")
+        second_layer(0, BLOCK, BLOCK, (0,), "bank2")
+        second_layer(0, 0, C, (1,), "bank6")
+        hidden.append(hidden_values(3, gate_sums((3,))[0]))
+        second_layer(0, 0, C, (2,), "bank0")
+        for block in range(HALVES, BLOCKS):
+            turn(block, hidden[block])
         quantise(1, 0, C)
-        second_layer(0, 0, C, (2, 3), "bank1")
-        second_layer(1, 0, C, (0, 1), "bank2")
+        second_layer(0, 0, C, (3,), "bank5")
+        second_layer(1, 0, C, (0, 1), "bank1")
         second_layer(1, 0, C, (2, 3), "bank3")
         for half in range(HALVES):
             scatter(0, half * BLOCK, BLOCK)

@@ -24,7 +24,7 @@ BLOCK = 128
 BLOCKS = SLOTS // BLOCK
 ROWS = N // P
 HALVES = C // BLOCK
-WINDOW = 704
+WARM_UP = 3
 GATE_BANKS = ("bank0", "bank2", "bank4", "bank0")
 UP_BANKS = ("bank1", "bank3", "bank5", "bank5")
 TURN_BANKS = ("bank1", "bank3", "bank7", "bank5")
@@ -56,8 +56,6 @@ def tile_moe_pkd_glu_gelu_kernel(
         nc.gpsimd.memset(x_plane[:].bitcast(I32), 0)
         for plane in (w1_plane, w3_plane):
             nc.vector.memset(plane[:].bitcast(I32), 0)
-        nothing = held.tile([P, 4 * H], BF16, name="nothing", align_bytes=64)
-        nc.gpsimd.memset(nothing[:].bitcast(I32), 0)
         identity = held.tile([P, P], F32, name="identity")
         make_identity(nc, identity[:])
         nc.gpsimd.memset(w2_plane[:].bitcast(I32), 0)
@@ -72,8 +70,7 @@ def tile_moe_pkd_glu_gelu_kernel(
             nc.sync.dma_start(codes[:].bitcast(I32), words[e].bitcast(I32).rearrange("s p w -> p s w"))
             return codes
 
-        tokens = [load_tokens(0, WINDOW)]
-        nc.vector.memset(tokens[0][:, T:WINDOW].bitcast(I32), 0)
+        tokens = [load_tokens(0, T)]
         nc.sync.dma_start(offsets[:], offs)
         load_scale_rows((nc.scalar, nc.sync), x_plane, x_scales, PASSES)
         tokens.append(load_tokens(1, T))
@@ -84,12 +81,14 @@ def tile_moe_pkd_glu_gelu_kernel(
         w3 = [load_words(w3_words, 0, "w3_0")]
         load_scale_rows((nc.sync,), w3_plane, w3_scales.rearrange("e s q i -> (e s) q i"), E * PASSES)
         w1.append(load_words(w1_words, 1, "w1_1"))
-        load_scale_rows((nc.sync,), w2_plane, w2_scales.rearrange("e s q n -> (e s) q n"), E)
-        w3.append(load_words(w3_words, 1, "w3_1"))
         w2 = held.tile([P, E, 2 * N], U8, name="w2", align_bytes=64)
-        nc.sync.dma_start(w2[:].bitcast(I32), w2_words.bitcast(I32).rearrange("e s p w -> p (e s) w"))
         gates = held.tile([P, SLOTS], F32, name="gates")
-        nc.sync.dma_start(gates[:], gate[0:P, :])
+
+        def load_late():
+            load_scale_rows((nc.sync,), w2_plane, w2_scales.rearrange("e s q n -> (e s) q n"), E)
+            w3.append(load_words(w3_words, 1, "w3_1"))
+            nc.sync.dma_start(w2[:].bitcast(I32), w2_words.bitcast(I32).rearrange("e s p w -> p (e s) w"))
+            nc.sync.dma_start(gates[:], gate[0:P, :])
 
         zero = held.tile([P, 1], F32, name="zero")
         nc.vector.memset(zero[:], 0.0)
@@ -142,7 +141,7 @@ def tile_moe_pkd_glu_gelu_kernel(
             b = psum.tile([P, H], F32, name=f"b{block}", tag=UP_BANKS[block])
             for o in range(PASSES):
                 multiply(b, block, o, w3, w3_plane)
-            product = held.tile([P, 2, P, 2], BF16, name=f"hidden{block}", align_bytes=64)
+            product = held.tile([P, 2, P, 2], BF16, name=f"hidden{block}", tag=f"hidden{block}", align_bytes=64)
             nc.vector.tensor_tensor(product[:], by_pairs(b), act[:], MULT)
             return product
 
@@ -169,7 +168,7 @@ def tile_moe_pkd_glu_gelu_kernel(
                 in_=grouped[e][:, 4 * first : 4 * (first + count)],
             )
 
-        def second_layer(e, first, count, rows, bank):
+        def second_layer(e, first, count, rows, bank, target=None):
             sums = psum.tile([P, len(rows), count], F32, name="y_bank", tag=bank)
             for j in rows:
                 nc.tensor.matmul_mx(
@@ -182,33 +181,27 @@ def tile_moe_pkd_glu_gelu_kernel(
                     stop=True,
                 )
             slot = e * C + first
-            nc.scalar.copy(y[:, rows[0] : rows[-1] + 1, slot : slot + count], sums[:])
+            nc.scalar.copy(y[:, rows[0] : rows[-1] + 1, slot : slot + count] if target is None else target, sums[:])
 
-        def scatter(j, slot, count):
+        def scatter(j, slot, count, values=None):
             cols = slice(slot, slot + count)
             entries = offsets[:, slot // 16 : (slot + count) // 16]
-            nc.vector.tensor_tensor(results[j][:].indirect(entries), y[:, j, cols], gates[:, cols], MULT)
+            nc.vector.tensor_tensor(results[j][:].indirect(entries), y[:, j, cols] if values is None else values, gates[:, cols], MULT)
 
-        idle_codes = held.tile([P, H], U32, name="idle_codes", align_bytes=64)
-        idle_bytes = held.tile([P, H], U8, name="idle_bytes", align_bytes=64)
-        nc.vector.quantize_mx(out=idle_codes[:].bitcast(FP8X4), scales=idle_bytes[:], in_=nothing[:])
+        for e in range(E):
+            nc.vector.tensor_copy(x_codes[0][:, e * C : (e + 1) * C], tokens[0][:].indirect(entries_of(e)))
         unread = psum.tile([P, H], F32, name="unread", tag="bank6")
-
-        def warm_up(codes):
-            for repeat in range(2):
-                nc.tensor.matmul_mx(
-                    out=unread[:],
-                    lhsT=codes[:, 0:P].bitcast(FP8X4),
-                    lhsT_scale=idle_bytes[:, 0:P],
-                    rhs=idle_codes[:, 0 : H // 2].bitcast(U8).bitcast(FP4X4),
-                    rhs_scale=idle_bytes[:],
-                    start=True,
-                    stop=True,
-                )
-
-        warm_up(idle_codes)
-        nc.vector.tensor_copy(x_codes[0][:], tokens[0][:].indirect(offsets[:]))
-        warm_up(x_codes[0])
+        for repeat in range(WARM_UP):
+            nc.tensor.matmul_mx(
+                out=unread[:],
+                lhsT=x_codes[0][:, 0:P].bitcast(FP8X4),
+                lhsT_scale=w2_plane[:, 0:P],
+                rhs=w2_plane[:, 0 : 2 * H].bitcast(FP4X4),
+                rhs_scale=w2_plane[:, 0:H],
+                start=True,
+                stop=True,
+            )
+        load_late()
         gather_bytes(0, "x_bytes0")
         for e in range(E):
             nc.vector.tensor_copy(x_codes[1][:, e * C : (e + 1) * C], tokens[1][:].indirect(entries_of(e)))
@@ -227,13 +220,16 @@ def tile_moe_pkd_glu_gelu_kernel(
         for block in range(HALVES, BLOCKS):
             turn(block, hidden[block])
         quantise(1, 0, C)
-        second_layer(0, 0, C, (3,), "bank5")
-        second_layer(1, 0, C, (0, 1), "bank1")
+        last_row = held.tile([P, 1, C], F32, name="last_row", tag="hidden3", align_bytes=64)
+        second_layer(0, 0, C, (3,), "bank2", last_row[:])
+        second_layer(1, 0, C, (0,), "bank1")
+        second_layer(1, 0, C, (1,), "bank4")
         second_layer(1, 0, C, (2, 3), "bank3")
         for half in range(HALVES):
             scatter(0, half * BLOCK, BLOCK)
-        for j in range(1, ROWS):
+        for j in range(1, ROWS - 1):
             scatter(j, 0, C)
+        scatter(ROWS - 1, 0, C, last_row[:, 0, :])
         for j in range(ROWS):
             scatter(j, C, C)
             nc.sync.dma_start(out[j * P : (j + 1) * P, :], results[j][:])

@@ -142,7 +142,13 @@ def tile_moe_pkd_glu_gelu_kernel(
             for o in range(PASSES):
                 multiply(b, block, o, w3, w3_plane)
             product = held.tile([P, 2, P, 2], BF16, name=f"hidden{block}", tag=f"hidden{block}", align_bytes=64)
-            nc.vector.tensor_tensor(product[:], by_pairs(b), act[:], MULT)
+            if block < BLOCKS - 1:
+                nc.vector.tensor_tensor(product[:], by_pairs(b), act[:], MULT)
+            else:
+                up = held.tile([P, 2, P, 2], F32, name="up", align_bytes=64)
+                nc.scalar.copy(up[:], by_pairs(b))
+                flat = "p u q v -> p (u q v)"
+                nc.gpsimd.tensor_tensor(product[:].rearrange(flat), up[:].rearrange(flat), act[:].rearrange(flat), MULT)
             return product
 
         grouped = [held.tile([P, 4 * C], BF16, name=f"grouped{e}", align_bytes=64) for e in range(E)]
@@ -181,6 +187,8 @@ def tile_moe_pkd_glu_gelu_kernel(
                     stop=True,
                 )
             slot = e * C + first
+            if target is False:
+                return sums
             nc.scalar.copy(y[:, rows[0] : rows[-1] + 1, slot : slot + count] if target is None else target, sums[:])
 
         def scatter(j, slot, count, values=None):
@@ -188,8 +196,8 @@ def tile_moe_pkd_glu_gelu_kernel(
             entries = offsets[:, slot // 16 : (slot + count) // 16]
             nc.vector.tensor_tensor(results[j][:].indirect(entries), y[:, j, cols] if values is None else values, gates[:, cols], MULT)
 
-        for e in range(E):
-            nc.vector.tensor_copy(x_codes[0][:, e * C : (e + 1) * C], tokens[0][:].indirect(entries_of(e)))
+        nc.vector.tensor_copy(x_codes[0][:, 0:BLOCK], tokens[0][:].indirect(offsets[:, 0 : BLOCK // 16]))
+        nc.vector.tensor_copy(x_codes[0][:, BLOCK:SLOTS], tokens[0][:].indirect(offsets[:, BLOCK // 16 : SLOTS // 16]))
         unread = psum.tile([P, H], F32, name="unread", tag="bank6")
         for repeat in range(WARM_UP):
             nc.tensor.matmul_mx(
@@ -214,7 +222,7 @@ def tile_moe_pkd_glu_gelu_kernel(
         hidden.append(hidden_values(2, gate_sums((2,))[0]))
         second_layer(0, 0, BLOCK, (0,), "bank0")
         second_layer(0, BLOCK, BLOCK, (0,), "bank2")
-        second_layer(0, 0, C, (1,), "bank6")
+        second_row = second_layer(0, 0, C, (1,), "bank6", False)
         hidden.append(hidden_values(3, gate_sums((3,))[0]))
         second_layer(0, 0, C, (2,), "bank0")
         for block in range(HALVES, BLOCKS):
@@ -225,10 +233,11 @@ def tile_moe_pkd_glu_gelu_kernel(
         second_layer(1, 0, C, (0,), "bank1")
         second_layer(1, 0, C, (1,), "bank4")
         second_layer(1, 0, C, (2, 3), "bank3")
-        for half in range(HALVES):
-            scatter(0, half * BLOCK, BLOCK)
-        for j in range(1, ROWS - 1):
-            scatter(j, 0, C)
+        scatter(0, 0, BLOCK)
+        nc.vector.tensor_tensor(y[:, 1, 0:C], second_row[:, 0, :], gates[:, 0:C], MULT)
+        scatter(0, BLOCK, BLOCK)
+        nc.vector.tensor_copy(results[1][:].indirect(entries_of(0)), y[:, 1, 0:C])
+        scatter(2, 0, C)
         scatter(ROWS - 1, 0, C, last_row[:, 0, :])
         for j in range(ROWS):
             scatter(j, C, C)

@@ -75,9 +75,8 @@ def tile_moe_pkd_glu_gelu_kernel(
         load_scale_rows((nc.scalar, nc.sync), x_plane, x_scales, PASSES)
         tokens.append(load_tokens(1, T))
         w1_rows = w1_scales.rearrange("e s q i -> (e s) q i")
-        load_scale_rows((nc.sync,), w1_plane, w1_rows, E * PASSES, (0, 1))
         w1 = [load_words(w1_words, 0, "w1_0")]
-        load_scale_rows((nc.sync,), w1_plane, w1_rows, E * PASSES, (2, 3))
+        load_scale_rows((nc.sync,), w1_plane, w1_rows, E * PASSES)
         w3 = [load_words(w3_words, 0, "w3_0")]
         load_scale_rows((nc.sync,), w3_plane, w3_scales.rearrange("e s q i -> (e s) q i"), E * PASSES)
         w1.append(load_words(w1_words, 1, "w1_1"))
@@ -106,19 +105,20 @@ def tile_moe_pkd_glu_gelu_kernel(
         x_codes = [held.tile([P, SLOTS], U32, name=f"x_codes{o}", align_bytes=64) for o in range(PASSES)]
         x_bytes = []
 
-        def gather_bytes(e, tag):
-            scales = held.tile([P, PASSES, C], U8, name=f"x_bytes{e}", tag=tag, align_bytes=64)
+        def gather_bytes(first, blocks, tag):
+            scales = held.tile([P, PASSES, blocks * BLOCK], U8, name=f"x_bytes{first}", tag=tag, align_bytes=64)
+            entries = offsets[:, first * BLOCK // 16 : (first + blocks) * BLOCK // 16]
             for o in range(PASSES):
-                nc.vector.tensor_copy(scales[:, o, :], x_plane[:, o * T : (o + 1) * T].indirect(entries_of(e)))
-            x_bytes.append(scales)
+                nc.vector.tensor_copy(scales[:, o, :], x_plane[:, o * T : (o + 1) * T].indirect(entries))
+            x_bytes.extend([[scales[:, o, i * BLOCK : (i + 1) * BLOCK] for o in range(PASSES)] for i in range(blocks)])
 
         def multiply(sums, block, o, words, plane):
-            e, half = divmod(block, HALVES)
+            e = block // HALVES
             at = (e * PASSES + o) * H
             nc.tensor.matmul_mx(
                 out=sums[:],
                 lhsT=x_codes[o][:, block * BLOCK : (block + 1) * BLOCK].bitcast(FP8X4),
-                lhsT_scale=x_bytes[e][:, o, half * BLOCK : (half + 1) * BLOCK],
+                lhsT_scale=x_bytes[block][o],
                 rhs=words[e][:, o, :].bitcast(FP4X4),
                 rhs_scale=plane[:, at : at + H],
                 start=(o == 0),
@@ -136,7 +136,7 @@ def tile_moe_pkd_glu_gelu_kernel(
             return bank[:].rearrange("p (q u v) -> p u q v", u=2, v=2)
 
         def hidden_values(block, a):
-            act = held.tile([P, 2, P, 2], F32, name=f"act{block}", align_bytes=64)
+            act = held.tile([P, 2, P, 2], F32, name=f"act{block}", tag=f"act{block}", align_bytes=64)
             nc.scalar.activation(act[:], by_pairs(a), GELU)
             b = psum.tile([P, H], F32, name=f"b{block}", tag=UP_BANKS[block])
             for o in range(PASSES):
@@ -210,12 +210,13 @@ def tile_moe_pkd_glu_gelu_kernel(
                 stop=True,
             )
         load_late()
-        gather_bytes(0, "x_bytes0")
+        gather_bytes(0, 2, "x_bytes0")
         for e in range(E):
             nc.vector.tensor_copy(x_codes[1][:, e * C : (e + 1) * C], tokens[1][:].indirect(entries_of(e)))
-        gather_bytes(1, "tokens1")
+        gather_bytes(2, 1, "tokens1")
 
         hidden = [hidden_values(block, a) for block, a in enumerate(gate_sums((0, 1)))]
+        gather_bytes(3, 1, "act1")
         for half in range(HALVES):
             turn(half, hidden[half])
             quantise(0, half * BLOCK, BLOCK)

@@ -72,7 +72,7 @@ def tile_moe_pkd_glu_gelu_kernel(
 
         tokens = [load_tokens(0, T)]
         nc.sync.dma_start(offsets[:], offs)
-        load_scale_rows((nc.scalar, nc.sync), x_plane, x_scales, PASSES)
+        load_scale_rows((nc.sync,), x_plane, x_scales, PASSES)
         tokens.append(load_tokens(1, T))
         w1_rows = w1_scales.rearrange("e s q i -> (e s) q i")
         w1 = [load_words(w1_words, 0, "w1_0")]

@@ -16,6 +16,7 @@ U8 = mybir.dt.uint8
 FP8X4 = mybir.dt.float8_e4m3fn_x4
 FP4X4 = mybir.dt.float4_e2m1fn_x4
 GELU = mybir.ActivationFunctionType.Gelu_apprx_tanh
+COPY = mybir.ActivationFunctionType.Copy
 MULT = mybir.AluOpType.mult
 
 P = 128
@@ -25,9 +26,9 @@ BLOCKS = SLOTS // BLOCK
 ROWS = N // P
 HALVES = C // BLOCK
 WARM_UP = 3
-GATE_BANKS = ("bank0", "bank2", "bank4", "bank0")
+GATE_BANKS = ("bank0", "bank2", "bank4", "bank6")
 UP_BANKS = ("bank1", "bank3", "bank5", "bank5")
-TURN_BANKS = ("bank1", "bank3", "bank7", "bank5")
+TURN_BANKS = ("bank1", "bank3")
 
 
 def load_scale_rows(queues, plane, rows, groups, which=range(4)):
@@ -97,7 +98,6 @@ def tile_moe_pkd_glu_gelu_kernel(
             window = held.tile([P, T], F32, name=f"result{j}")
             nc.scalar.activation(window[:], zero[:].to_broadcast([P, T]), GELU)
             results.append(window)
-        y = held.tile([P, ROWS, SLOTS], F32, name="y")
 
         def entries_of(e):
             return offsets[:, e * C // 16 : (e + 1) * C // 16]
@@ -142,13 +142,7 @@ def tile_moe_pkd_glu_gelu_kernel(
             for o in range(PASSES):
                 multiply(b, block, o, w3, w3_plane)
             product = held.tile([P, 2, P, 2], BF16, name=f"hidden{block}", tag=f"hidden{block}", align_bytes=64)
-            if block < BLOCKS - 1:
-                nc.vector.tensor_tensor(product[:], by_pairs(b), act[:], MULT)
-            else:
-                up = held.tile([P, 2, P, 2], F32, name="up", align_bytes=64)
-                nc.scalar.copy(up[:], by_pairs(b))
-                flat = "p u q v -> p (u q v)"
-                nc.gpsimd.tensor_tensor(product[:].rearrange(flat), up[:].rearrange(flat), act[:].rearrange(flat), MULT)
+            nc.vector.tensor_tensor(product[:], by_pairs(b), act[:], MULT)
             return product
 
         grouped = [held.tile([P, 4 * C], BF16, name=f"grouped{e}", align_bytes=64) for e in range(E)]
@@ -174,27 +168,42 @@ def tile_moe_pkd_glu_gelu_kernel(
                 in_=grouped[e][:, 4 * first : 4 * (first + count)],
             )
 
-        def second_layer(e, first, count, rows, bank, target=None):
-            sums = psum.tile([P, len(rows), count], F32, name="y_bank", tag=bank)
-            for j in rows:
+        def second_layer(e, rows, bank, tag):
+            sums = psum.tile([P, len(rows), C], F32, name="y_bank", tag=bank)
+            for at, j in enumerate(rows):
                 nc.tensor.matmul_mx(
-                    out=sums[:, j - rows[0], :],
+                    out=sums[:, at, :],
                     lhsT=w2[:, e, 2 * j * P : 2 * (j + 1) * P].bitcast(FP4X4),
                     lhsT_scale=w2_plane[:, e * N + j * P : e * N + (j + 1) * P],
-                    rhs=h_codes[e][:, first : first + count].bitcast(FP8X4),
-                    rhs_scale=h_bytes[e][:, first : first + count],
+                    rhs=h_codes[e][:].bitcast(FP8X4),
+                    rhs_scale=h_bytes[e][:],
                     start=True,
                     stop=True,
                 )
-            slot = e * C + first
-            if target is False:
-                return sums
-            nc.scalar.copy(y[:, rows[0] : rows[-1] + 1, slot : slot + count] if target is None else target, sums[:])
+            gated = held.tile([P, len(rows), C], F32, name=f"gated{e}_{rows[0]}", tag=tag, align_bytes=64)
+            weights = gates[:, e * C : (e + 1) * C].unsqueeze(1).to_broadcast([P, len(rows), C])
+            nc.vector.tensor_tensor(gated[:], sums[:], weights, MULT)
+            return {j: gated[:, at, :] for at, j in enumerate(rows)}
 
-        def scatter(j, slot, count, values=None):
-            cols = slice(slot, slot + count)
-            entries = offsets[:, slot // 16 : (slot + count) // 16]
-            nc.vector.tensor_tensor(results[j][:].indirect(entries), y[:, j, cols] if values is None else values, gates[:, cols], MULT)
+        def scatter_on_scalar(j, e, values):
+            nc.scalar.activation(results[j][:].indirect(entries_of(e)), values[j], COPY)
+
+        def scatter_on_vector(j, e, values):
+            nc.vector.tensor_copy(results[j][:].indirect(entries_of(e)), values[j])
+
+        def store(j):
+            nc.sync.dma_start(out[j * P : (j + 1) * P, :], results[j][:])
+
+        def turn_second_expert(hidden):
+            turned = psum.tile([P, HALVES, 2, BLOCK], F32, name="turned_late", tag="bank7")
+            for half in range(HALVES):
+                pairs = hidden[HALVES + half][:].rearrange("p u q v -> p (u q v)").bitcast(F32)
+                for u in range(2):
+                    nc.tensor.transpose(turned[:, half, u, :], pairs[:, u * P : (u + 1) * P], identity[:])
+            nc.vector.tensor_copy(
+                grouped[1][:].bitcast(F32).rearrange("p (h r u) -> p h r u", h=HALVES, u=2),
+                turned[:].rearrange("p h u r -> p h r u"),
+            )
 
         nc.vector.tensor_copy(x_codes[0][:, 0:BLOCK], tokens[0][:].indirect(offsets[:, 0 : BLOCK // 16]))
         nc.vector.tensor_copy(x_codes[0][:, BLOCK:SLOTS], tokens[0][:].indirect(offsets[:, BLOCK // 16 : SLOTS // 16]))
@@ -221,25 +230,20 @@ def tile_moe_pkd_glu_gelu_kernel(
             turn(half, hidden[half])
             quantise(0, half * BLOCK, BLOCK)
         hidden.append(hidden_values(2, gate_sums((2,))[0]))
-        second_layer(0, 0, BLOCK, (0,), "bank0")
-        second_layer(0, BLOCK, BLOCK, (0,), "bank2")
-        second_row = second_layer(0, 0, C, (1,), "bank6", False)
+        first = second_layer(0, (1,), "bank0", "gated_a")
+        scatter_on_scalar(1, 0, first)
+        first = {**first, **second_layer(0, (2, 3), "bank2", "gated_b")}
         hidden.append(hidden_values(3, gate_sums((3,))[0]))
-        second_layer(0, 0, C, (2,), "bank0")
-        for block in range(HALVES, BLOCKS):
-            turn(block, hidden[block])
+        scatter_on_scalar(2, 0, first)
+        scatter_on_scalar(3, 0, first)
+        turn_second_expert(hidden)
+        first = {**first, **second_layer(0, (0,), "bank1", "hidden3")}
         quantise(1, 0, C)
-        last_row = held.tile([P, 1, C], F32, name="last_row", tag="hidden3", align_bytes=64)
-        second_layer(0, 0, C, (3,), "bank2", last_row[:])
-        second_layer(1, 0, C, (0,), "bank1")
-        second_layer(1, 0, C, (1,), "bank4")
-        second_layer(1, 0, C, (2, 3), "bank3")
-        scatter(0, 0, BLOCK)
-        nc.vector.tensor_tensor(y[:, 1, 0:C], second_row[:, 0, :], gates[:, 0:C], MULT)
-        scatter(0, BLOCK, BLOCK)
-        nc.vector.tensor_copy(results[1][:].indirect(entries_of(0)), y[:, 1, 0:C])
-        scatter(2, 0, C)
-        scatter(ROWS - 1, 0, C, last_row[:, 0, :])
-        for j in range(ROWS):
-            scatter(j, C, C)
-            nc.sync.dma_start(out[j * P : (j + 1) * P, :], results[j][:])
+        scatter_on_vector(0, 0, first)
+        second = second_layer(1, (2, 3), "bank3", "gated_c")
+        second = {**second, **second_layer(1, (0, 1), "bank4", "gated_d")}
+        for j in range(2):
+            scatter_on_vector(j, 1, second)
+            scatter_on_scalar(2 + j, 1, second)
+            store(j)
+            store(2 + j)

@@ -25,10 +25,10 @@ BLOCK = 128
 BLOCKS = SLOTS // BLOCK
 ROWS = N // P
 HALVES = C // BLOCK
-WARM_UP = 3
+WARM_UP = 2
 GATE_BANKS = ("bank0", "bank2", "bank4", "bank6")
-UP_BANKS = ("bank1", "bank3", "bank5", "bank5")
-TURN_BANKS = ("bank1", "bank3")
+UP_BANKS = ("bank1", "bank3", "bank5", "bank2")
+TURN_BANKS = ("bank1", "bank3", "bank7", "bank5")
 
 
 def load_scale_rows(queues, plane, rows, groups, which=range(4)):
@@ -74,8 +74,8 @@ def tile_moe_pkd_glu_gelu_kernel(
         tokens = [load_tokens(0, T)]
         nc.sync.dma_start(offsets[:], offs)
         load_scale_rows((nc.sync,), x_plane, x_scales, PASSES)
-        tokens.append(load_tokens(1, T))
         w1_rows = w1_scales.rearrange("e s q i -> (e s) q i")
+        tokens.append(load_tokens(1, T))
         w1 = [load_words(w1_words, 0, "w1_0")]
         load_scale_rows((nc.sync,), w1_plane, w1_rows, E * PASSES)
         w3 = [load_words(w3_words, 0, "w3_0")]
@@ -85,8 +85,8 @@ def tile_moe_pkd_glu_gelu_kernel(
         gates = held.tile([P, SLOTS], F32, name="gates")
 
         def load_late():
-            load_scale_rows((nc.sync,), w2_plane, w2_scales.rearrange("e s q n -> (e s) q n"), E)
             w3.append(load_words(w3_words, 1, "w3_1"))
+            load_scale_rows((nc.sync,), w2_plane, w2_scales.rearrange("e s q n -> (e s) q n"), E)
             nc.sync.dma_start(w2[:].bitcast(I32), w2_words.bitcast(I32).rearrange("e s p w -> p (e s) w"))
             nc.sync.dma_start(gates[:], gate[0:P, :])
 
@@ -153,7 +153,8 @@ def tile_moe_pkd_glu_gelu_kernel(
             turned = psum.tile([P, 2, BLOCK], F32, name=f"turned{block}", tag=TURN_BANKS[block])
             for u in range(2):
                 nc.tensor.transpose(turned[:, u, :], pairs[:, u * P : (u + 1) * P], identity[:])
-            nc.scalar.copy(
+            copy = nc.vector.tensor_copy if block == BLOCKS - 1 else nc.scalar.copy
+            copy(
                 grouped[e][:, 4 * half * BLOCK : 4 * (half + 1) * BLOCK].bitcast(F32).rearrange("p (r u) -> p r u", u=2),
                 turned[:].rearrange("p u r -> p r u"),
             )
@@ -168,7 +169,7 @@ def tile_moe_pkd_glu_gelu_kernel(
                 in_=grouped[e][:, 4 * first : 4 * (first + count)],
             )
 
-        def second_layer(e, rows, bank, tag):
+        def second_layer(e, rows, bank, tag, gate_now=True):
             sums = psum.tile([P, len(rows), C], F32, name="y_bank", tag=bank)
             for at, j in enumerate(rows):
                 nc.tensor.matmul_mx(
@@ -181,8 +182,11 @@ def tile_moe_pkd_glu_gelu_kernel(
                     stop=True,
                 )
             gated = held.tile([P, len(rows), C], F32, name=f"gated{e}_{rows[0]}", tag=tag, align_bytes=64)
-            weights = gates[:, e * C : (e + 1) * C].unsqueeze(1).to_broadcast([P, len(rows), C])
-            nc.vector.tensor_tensor(gated[:], sums[:], weights, MULT)
+            if gate_now:
+                weights = gates[:, e * C : (e + 1) * C].unsqueeze(1).to_broadcast([P, len(rows), C])
+                nc.vector.tensor_tensor(gated[:], sums[:], weights, MULT)
+            else:
+                nc.scalar.copy(gated[:], sums[:])
             return {j: gated[:, at, :] for at, j in enumerate(rows)}
 
         def scatter_on_scalar(j, e, values):
@@ -192,29 +196,20 @@ def tile_moe_pkd_glu_gelu_kernel(
             nc.vector.tensor_copy(results[j][:].indirect(entries_of(e)), values[j])
 
         def store(j):
-            nc.sync.dma_start(out[j * P : (j + 1) * P, :], results[j][:])
+            queue = nc.scalar if j == ROWS - 1 else nc.sync
+            queue.dma_start(out[j * P : (j + 1) * P, :], results[j][:])
 
-        def turn_second_expert(hidden):
-            turned = psum.tile([P, HALVES, 2, BLOCK], F32, name="turned_late", tag="bank7")
-            for half in range(HALVES):
-                pairs = hidden[HALVES + half][:].rearrange("p u q v -> p (u q v)").bitcast(F32)
-                for u in range(2):
-                    nc.tensor.transpose(turned[:, half, u, :], pairs[:, u * P : (u + 1) * P], identity[:])
-            nc.vector.tensor_copy(
-                grouped[1][:].bitcast(F32).rearrange("p (h r u) -> p h r u", h=HALVES, u=2),
-                turned[:].rearrange("p h u r -> p h r u"),
-            )
-
-        nc.vector.tensor_copy(x_codes[0][:, 0:BLOCK], tokens[0][:].indirect(offsets[:, 0 : BLOCK // 16]))
-        nc.vector.tensor_copy(x_codes[0][:, BLOCK:SLOTS], tokens[0][:].indirect(offsets[:, BLOCK // 16 : SLOTS // 16]))
+        for e in range(E):
+            nc.vector.tensor_copy(x_codes[0][:, e * C : (e + 1) * C], tokens[0][:].indirect(entries_of(e)))
         unread = psum.tile([P, H], F32, name="unread", tag="bank6")
+        first_bytes = x_codes[0][:, 0:C].bitcast(U8)
         for repeat in range(WARM_UP):
             nc.tensor.matmul_mx(
                 out=unread[:],
-                lhsT=x_codes[0][:, 0:P].bitcast(FP8X4),
-                lhsT_scale=w2_plane[:, 0:P],
-                rhs=w2_plane[:, 0 : 2 * H].bitcast(FP4X4),
-                rhs_scale=w2_plane[:, 0:H],
+                lhsT=x_codes[0][:, 0:BLOCK].bitcast(FP8X4),
+                lhsT_scale=first_bytes[:, 0:P],
+                rhs=first_bytes.bitcast(FP4X4),
+                rhs_scale=first_bytes[:, 0:H],
                 start=True,
                 stop=True,
             )
@@ -226,24 +221,26 @@ def tile_moe_pkd_glu_gelu_kernel(
 
         hidden = [hidden_values(block, a) for block, a in enumerate(gate_sums((0, 1)))]
         gather_bytes(3, 1, "act1")
-        for half in range(HALVES):
-            turn(half, hidden[half])
-            quantise(0, half * BLOCK, BLOCK)
         hidden.append(hidden_values(2, gate_sums((2,))[0]))
-        first = second_layer(0, (1,), "bank0", "gated_a")
-        scatter_on_scalar(1, 0, first)
-        first = {**first, **second_layer(0, (2, 3), "bank2", "gated_b")}
+        turn(0, hidden[0])
+        turn(1, hidden[1])
+        quantise(0, 0, C)
         hidden.append(hidden_values(3, gate_sums((3,))[0]))
+        turn(2, hidden[2])
+        first = second_layer(0, (1,), "bank0", "gated_a")
+        plain = second_layer(0, (0,), "bank1", "plain", False)
+        scatter_on_scalar(1, 0, first)
+        first = {**first, **second_layer(0, (2,), "bank4", "gated_b")}
         scatter_on_scalar(2, 0, first)
-        scatter_on_scalar(3, 0, first)
-        turn_second_expert(hidden)
-        first = {**first, **second_layer(0, (0,), "bank1", "hidden3")}
+        turn(3, hidden[3])
         quantise(1, 0, C)
-        scatter_on_vector(0, 0, first)
-        second = second_layer(1, (2, 3), "bank3", "gated_c")
-        second = {**second, **second_layer(1, (0, 1), "bank4", "gated_d")}
+        first = {**first, **second_layer(0, (3,), "bank3", "gated_f")}
+        scatter_on_scalar(3, 0, first)
+        nc.vector.tensor_tensor(results[0][:].indirect(entries_of(0)), plain[0], gates[:, 0:C], MULT)
+        second = second_layer(1, (2, 3), "bank2", "gated_c")
+        second = {**second, **second_layer(1, (0, 1), "bank6", "gated_d")}
         for j in range(2):
-            scatter_on_vector(j, 1, second)
             scatter_on_scalar(2 + j, 1, second)
-            store(j)
             store(2 + j)
+            scatter_on_vector(j, 1, second)
+            store(j)

@@ -26,9 +26,9 @@ BLOCKS = SLOTS // BLOCK
 ROWS = N // P
 HALVES = C // BLOCK
 WARM_UP = 2
-GATE_BANKS = ("bank0", "bank2", "bank4", "bank6")
+GATE_BANKS = ("bank0", "bank2", "bank4", "bank3")
 UP_BANKS = ("bank1", "bank3", "bank5", "bank2")
-TURN_BANKS = ("bank1", "bank3", "bank7", "bank5")
+TURN_BANKS = ("bank6", "bank1", "bank7", "bank5")
 
 
 def load_scale_rows(queues, plane, rows, groups, which=range(4)):
@@ -103,14 +103,16 @@ def tile_moe_pkd_glu_gelu_kernel(
             return offsets[:, e * C // 16 : (e + 1) * C // 16]
 
         x_codes = [held.tile([P, SLOTS], U32, name=f"x_codes{o}", align_bytes=64) for o in range(PASSES)]
-        x_bytes = []
+        x_bytes = {}
 
-        def gather_bytes(first, blocks, tag):
-            scales = held.tile([P, PASSES, blocks * BLOCK], U8, name=f"x_bytes{first}", tag=tag, align_bytes=64)
+        def byte_tile(blocks, tag):
+            return held.tile([P, blocks * BLOCK], U8, name=f"bytes_{tag}", tag=tag, align_bytes=64)
+
+        def gather_bytes(o, first, blocks, scales):
             entries = offsets[:, first * BLOCK // 16 : (first + blocks) * BLOCK // 16]
-            for o in range(PASSES):
-                nc.vector.tensor_copy(scales[:, o, :], x_plane[:, o * T : (o + 1) * T].indirect(entries))
-            x_bytes.extend([[scales[:, o, i * BLOCK : (i + 1) * BLOCK] for o in range(PASSES)] for i in range(blocks)])
+            nc.vector.tensor_copy(scales, x_plane[:, o * T : (o + 1) * T].indirect(entries))
+            for i in range(blocks):
+                x_bytes.setdefault((first + i, o), scales[:, i * BLOCK : (i + 1) * BLOCK])
 
         def multiply(sums, block, o, words, plane):
             e = block // HALVES
@@ -118,7 +120,7 @@ def tile_moe_pkd_glu_gelu_kernel(
             nc.tensor.matmul_mx(
                 out=sums[:],
                 lhsT=x_codes[o][:, block * BLOCK : (block + 1) * BLOCK].bitcast(FP8X4),
-                lhsT_scale=x_bytes[block][o],
+                lhsT_scale=x_bytes[(block, o)],
                 rhs=words[e][:, o, :].bitcast(FP4X4),
                 rhs_scale=plane[:, at : at + H],
                 start=(o == 0),
@@ -214,13 +216,16 @@ def tile_moe_pkd_glu_gelu_kernel(
                 stop=True,
             )
         load_late()
-        gather_bytes(0, 2, "x_bytes0")
+        for o in range(PASSES):
+            gather_bytes(o, 0, 2, byte_tile(2, f"x_bytes{o}")[:])
         for e in range(E):
             nc.vector.tensor_copy(x_codes[1][:, e * C : (e + 1) * C], tokens[1][:].indirect(entries_of(e)))
-        gather_bytes(2, 1, "tokens1")
+        behind_words = byte_tile(3, "tokens1")
+        gather_bytes(0, 2, 2, behind_words[:, 0:C])
+        gather_bytes(1, 2, 1, behind_words[:, C : C + BLOCK])
 
         hidden = [hidden_values(block, a) for block, a in enumerate(gate_sums((0, 1)))]
-        gather_bytes(3, 1, "act1")
+        gather_bytes(1, 3, 1, byte_tile(1, "act1")[:])
         hidden.append(hidden_values(2, gate_sums((2,))[0]))
         turn(0, hidden[0])
         turn(1, hidden[1])
@@ -228,19 +233,23 @@ def tile_moe_pkd_glu_gelu_kernel(
         hidden.append(hidden_values(3, gate_sums((3,))[0]))
         turn(2, hidden[2])
         first = second_layer(0, (1,), "bank0", "gated_a")
-        plain = second_layer(0, (0,), "bank1", "plain", False)
+        plain = second_layer(0, (0,), "bank6", "plain", False)
         scatter_on_scalar(1, 0, first)
         first = {**first, **second_layer(0, (2,), "bank4", "gated_b")}
         scatter_on_scalar(2, 0, first)
         turn(3, hidden[3])
         quantise(1, 0, C)
-        first = {**first, **second_layer(0, (3,), "bank3", "gated_f")}
+        first = {**first, **second_layer(0, (3,), "bank1", "gated_f")}
         scatter_on_scalar(3, 0, first)
         nc.vector.tensor_tensor(results[0][:].indirect(entries_of(0)), plain[0], gates[:, 0:C], MULT)
-        second = second_layer(1, (2, 3), "bank2", "gated_c")
-        second = {**second, **second_layer(1, (0, 1), "bank6", "gated_d")}
-        for j in range(2):
-            scatter_on_scalar(2 + j, 1, second)
-            store(2 + j)
-            scatter_on_vector(j, 1, second)
-            store(j)
+        second = second_layer(1, (0,), "bank3", "gated_d")
+        second = {**second, **second_layer(1, (2, 3), "bank2", "gated_c")}
+        late = second_layer(1, (1,), "bank4", "late", False)
+        scatter_on_scalar(2, 1, second)
+        store(2)
+        scatter_on_vector(0, 1, second)
+        store(0)
+        scatter_on_scalar(3, 1, second)
+        store(3)
+        nc.vector.tensor_tensor(results[1][:].indirect(entries_of(1)), late[1], gates[:, C : 2 * C], MULT)
+        store(1)

@@ -242,14 +242,10 @@ def tile_moe_pkd_glu_gelu_kernel(
         first = {**first, **second_layer(0, (3,), "bank1", "gated_f")}
         scatter_on_scalar(3, 0, first)
         nc.vector.tensor_tensor(results[0][:].indirect(entries_of(0)), plain[0], gates[:, 0:C], MULT)
-        second = second_layer(1, (0,), "bank3", "gated_d")
+        second = second_layer(1, (0, 1), "bank3", "gated_d")
         second = {**second, **second_layer(1, (2, 3), "bank2", "gated_c")}
-        late = second_layer(1, (1,), "bank4", "late", False)
-        scatter_on_scalar(2, 1, second)
-        store(2)
-        scatter_on_vector(0, 1, second)
-        store(0)
-        scatter_on_scalar(3, 1, second)
-        store(3)
-        nc.vector.tensor_tensor(results[1][:].indirect(entries_of(1)), late[1], gates[:, C : 2 * C], MULT)
-        store(1)
+        for j in range(2):
+            scatter_on_scalar(2 + j, 1, second)
+            store(2 + j)
+            scatter_on_vector(j, 1, second)
+            store(j)

@@ -25,7 +25,7 @@ BLOCK = 128
 BLOCKS = SLOTS // BLOCK
 ROWS = N // P
 HALVES = C // BLOCK
-WARM_UP = 2
+WARM_UP = 4
 GATE_BANKS = ("bank0", "bank2", "bank4", "bank3")
 UP_BANKS = ("bank1", "bank3", "bank5", "bank2")
 TURN_BANKS = ("bank6", "bank1", "bank7", "bank5")
@@ -201,17 +201,17 @@ def tile_moe_pkd_glu_gelu_kernel(
             queue = nc.scalar if j == ROWS - 1 else nc.sync
             queue.dma_start(out[j * P : (j + 1) * P, :], results[j][:])
 
-        for e in range(E):
-            nc.vector.tensor_copy(x_codes[0][:, e * C : (e + 1) * C], tokens[0][:].indirect(entries_of(e)))
-        unread = psum.tile([P, H], F32, name="unread", tag="bank6")
-        first_bytes = x_codes[0][:, 0:C].bitcast(U8)
+        nc.vector.tensor_copy(x_codes[0][:, 0:BLOCK], tokens[0][:].indirect(offsets[:, 0 : BLOCK // 16]))
+        nc.vector.tensor_copy(x_codes[0][:, BLOCK:SLOTS], tokens[0][:].indirect(offsets[:, BLOCK // 16 : SLOTS // 16]))
+        unread = psum.tile([P, C], F32, name="unread", tag="bank6")
+        first_bytes = x_codes[0][:, 0:BLOCK].bitcast(U8)
         for repeat in range(WARM_UP):
             nc.tensor.matmul_mx(
                 out=unread[:],
                 lhsT=x_codes[0][:, 0:BLOCK].bitcast(FP8X4),
                 lhsT_scale=first_bytes[:, 0:P],
                 rhs=first_bytes.bitcast(FP4X4),
-                rhs_scale=first_bytes[:, 0:H],
+                rhs_scale=first_bytes[:, 0:C],
                 start=True,
                 stop=True,
             )

@@ -22,19 +22,21 @@ MULT = mybir.AluOpType.mult
 P = 128
 PASSES = K // 512
 BLOCK = 128
-BLOCKS = SLOTS // BLOCK
-ROWS = N // P
+LAST_BLOCK = SLOTS // BLOCK - 1
 HALVES = C // BLOCK
-WARM_UP = 4
+ROWS = N // P
+PER_COLUMN = 16
+WARM_UP = 2
+
 GATE_BANKS = ("bank0", "bank2", "bank4", "bank3")
 UP_BANKS = ("bank1", "bank3", "bank5", "bank2")
 TURN_BANKS = ("bank6", "bank1", "bank7", "bank5")
 
 
-def load_scale_rows(queues, plane, rows, groups, which=range(4)):
+def load_scale_rows(nc, plane, rows, groups):
     words = rows.bitcast(I32)
-    for r in which:
-        queues[r % len(queues)].dma_start(
+    for r in range(4):
+        nc.sync.dma_start(
             out=plane[r:P:32, :].bitcast(I32).rearrange("p (g w) -> p g w", g=groups),
             in_=words[:, r:16:4, :].rearrange("g q w -> q g w"),
         )
@@ -48,7 +50,7 @@ def tile_moe_pkd_glu_gelu_kernel(
         held = ctx.enter_context(tc.tile_pool(name="held", bufs=1))
         psum = ctx.enter_context(tc.psum_pool(name="psum", bufs=1))
 
-        offsets = held.tile([P, SLOTS // 16], U16, name="offsets")
+        offsets = held.tile([P, SLOTS // PER_COLUMN], U16, name="offsets")
 
         x_plane = held.tile([P, PASSES * T], U8, name="x_plane", align_bytes=64)
         w1_plane = held.tile([P, E * PASSES * H], U8, name="w1_plane", align_bytes=64)
@@ -61,9 +63,9 @@ def tile_moe_pkd_glu_gelu_kernel(
         make_identity(nc, identity[:])
         nc.gpsimd.memset(w2_plane[:].bitcast(I32), 0)
 
-        def load_tokens(o, columns):
-            table = held.tile([P, columns], U32, name=f"tokens{o}", tag=f"tokens{o}", align_bytes=64)
-            nc.sync.dma_start(table[:, 0:T].bitcast(I32), x_words[o].rearrange("p t r -> p (t r)").bitcast(I32))
+        def load_tokens(o):
+            table = held.tile([P, T], U32, name=f"tokens{o}", tag=f"tokens{o}", align_bytes=64)
+            nc.sync.dma_start(table[:].bitcast(I32), x_words[o].rearrange("p t r -> p (t r)").bitcast(I32))
             return table
 
         def load_words(words, e, name):
@@ -71,48 +73,48 @@ def tile_moe_pkd_glu_gelu_kernel(
             nc.sync.dma_start(codes[:].bitcast(I32), words[e].bitcast(I32).rearrange("s p w -> p s w"))
             return codes
 
-        tokens = [load_tokens(0, T)]
+        tokens = [load_tokens(0)]
         nc.sync.dma_start(offsets[:], offs)
-        load_scale_rows((nc.sync,), x_plane, x_scales, PASSES)
-        w1_rows = w1_scales.rearrange("e s q i -> (e s) q i")
-        tokens.append(load_tokens(1, T))
+        load_scale_rows(nc, x_plane, x_scales, PASSES)
+        tokens.append(load_tokens(1))
         w1 = [load_words(w1_words, 0, "w1_0")]
-        load_scale_rows((nc.sync,), w1_plane, w1_rows, E * PASSES)
+        load_scale_rows(nc, w1_plane, w1_scales.rearrange("e s q i -> (e s) q i"), E * PASSES)
         w3 = [load_words(w3_words, 0, "w3_0")]
-        load_scale_rows((nc.sync,), w3_plane, w3_scales.rearrange("e s q i -> (e s) q i"), E * PASSES)
+        load_scale_rows(nc, w3_plane, w3_scales.rearrange("e s q i -> (e s) q i"), E * PASSES)
         w1.append(load_words(w1_words, 1, "w1_1"))
+        w3.append(load_words(w3_words, 1, "w3_1"))
+        load_scale_rows(nc, w2_plane, w2_scales.rearrange("e s q n -> (e s) q n"), E)
         w2 = held.tile([P, E, 2 * N], U8, name="w2", align_bytes=64)
+        nc.sync.dma_start(w2[:].bitcast(I32), w2_words.bitcast(I32).rearrange("e s p w -> p (e s) w"))
         gates = held.tile([P, SLOTS], F32, name="gates")
-
-        def load_late():
-            w3.append(load_words(w3_words, 1, "w3_1"))
-            load_scale_rows((nc.sync,), w2_plane, w2_scales.rearrange("e s q n -> (e s) q n"), E)
-            nc.sync.dma_start(w2[:].bitcast(I32), w2_words.bitcast(I32).rearrange("e s p w -> p (e s) w"))
-            nc.sync.dma_start(gates[:], gate[0:P, :])
+        nc.sync.dma_start(gates[:], gate[0:P, :])
 
         zero = held.tile([P, 1], F32, name="zero")
         nc.vector.memset(zero[:], 0.0)
-
-        results = []
+        windows = []
         for j in range(ROWS):
-            window = held.tile([P, T], F32, name=f"result{j}")
+            window = held.tile([P, T], F32, name=f"window{j}")
             nc.scalar.activation(window[:], zero[:].to_broadcast([P, T]), GELU)
-            results.append(window)
+            windows.append(window)
 
-        def entries_of(e):
-            return offsets[:, e * C // 16 : (e + 1) * C // 16]
+        def entries(slot, count):
+            return offsets[:, slot // PER_COLUMN : (slot + count) // PER_COLUMN]
 
         x_codes = [held.tile([P, SLOTS], U32, name=f"x_codes{o}", align_bytes=64) for o in range(PASSES)]
         x_bytes = {}
 
+        def gather_words(o):
+            for e in range(E):
+                nc.vector.tensor_copy(x_codes[o][:, e * C : (e + 1) * C], tokens[o][:].indirect(entries(e * C, C)))
+
         def byte_tile(blocks, tag):
             return held.tile([P, blocks * BLOCK], U8, name=f"bytes_{tag}", tag=tag, align_bytes=64)
 
-        def gather_bytes(o, first, blocks, scales):
-            entries = offsets[:, first * BLOCK // 16 : (first + blocks) * BLOCK // 16]
-            nc.vector.tensor_copy(scales, x_plane[:, o * T : (o + 1) * T].indirect(entries))
-            for i in range(blocks):
-                x_bytes.setdefault((first + i, o), scales[:, i * BLOCK : (i + 1) * BLOCK])
+        def gather_bytes(o, first_block, blocks, target):
+            picked = entries(first_block * BLOCK, blocks * BLOCK)
+            nc.vector.tensor_copy(target, x_plane[:, o * T : (o + 1) * T].indirect(picked))
+            for b in range(blocks):
+                x_bytes.setdefault((first_block + b, o), target[:, b * BLOCK : (b + 1) * BLOCK])
 
         def multiply(sums, block, o, words, plane):
             e = block // HALVES
@@ -138,24 +140,27 @@ def tile_moe_pkd_glu_gelu_kernel(
             return bank[:].rearrange("p (q u v) -> p u q v", u=2, v=2)
 
         def hidden_values(block, a):
+            parts = (slice(0, 1), slice(1, 2)) if block == LAST_BLOCK else (slice(0, 2),)
             act = held.tile([P, 2, P, 2], F32, name=f"act{block}", tag=f"act{block}", align_bytes=64)
-            nc.scalar.activation(act[:], by_pairs(a), GELU)
+            for part in parts:
+                nc.scalar.activation(act[:, part], by_pairs(a)[:, part], GELU)
             b = psum.tile([P, H], F32, name=f"b{block}", tag=UP_BANKS[block])
             for o in range(PASSES):
                 multiply(b, block, o, w3, w3_plane)
-            product = held.tile([P, 2, P, 2], BF16, name=f"hidden{block}", tag=f"hidden{block}", align_bytes=64)
-            nc.vector.tensor_tensor(product[:], by_pairs(b), act[:], MULT)
+            product = held.tile([P, 2, P, 2], BF16, name=f"hidden{block}", align_bytes=64)
+            for part in parts:
+                nc.vector.tensor_tensor(product[:, part], by_pairs(b)[:, part], act[:, part], MULT)
             return product
 
         grouped = [held.tile([P, 4 * C], BF16, name=f"grouped{e}", align_bytes=64) for e in range(E)]
 
-        def turn(block, hidden):
+        def turn(block, values):
             e, half = divmod(block, HALVES)
-            pairs = hidden[:].rearrange("p u q v -> p (u q v)").bitcast(F32)
+            pairs = values[:].rearrange("p u q v -> p (u q v)").bitcast(F32)
             turned = psum.tile([P, 2, BLOCK], F32, name=f"turned{block}", tag=TURN_BANKS[block])
             for u in range(2):
                 nc.tensor.transpose(turned[:, u, :], pairs[:, u * P : (u + 1) * P], identity[:])
-            copy = nc.vector.tensor_copy if block == BLOCKS - 1 else nc.scalar.copy
+            copy = nc.vector.tensor_copy if block == LAST_BLOCK else nc.scalar.copy
             copy(
                 grouped[e][:, 4 * half * BLOCK : 4 * (half + 1) * BLOCK].bitcast(F32).rearrange("p (r u) -> p r u", u=2),
                 turned[:].rearrange("p u r -> p r u"),
@@ -164,64 +169,55 @@ def tile_moe_pkd_glu_gelu_kernel(
         h_codes = [held.tile([P, C], U32, name=f"h_codes{e}", align_bytes=64) for e in range(E)]
         h_bytes = [held.tile([P, C], U8, name=f"h_bytes{e}", align_bytes=64) for e in range(E)]
 
-        def quantise(e, first, count):
-            nc.vector.quantize_mx(
-                out=h_codes[e][:, first : first + count].bitcast(FP8X4),
-                scales=h_bytes[e][:, first : first + count],
-                in_=grouped[e][:, 4 * first : 4 * (first + count)],
-            )
+        def quantise(e):
+            nc.vector.quantize_mx(out=h_codes[e][:].bitcast(FP8X4), scales=h_bytes[e][:], in_=grouped[e][:])
 
-        def second_layer(e, rows, bank, tag, gate_now=True):
-            sums = psum.tile([P, len(rows), C], F32, name="y_bank", tag=bank)
+        def y_sums(rows, slot, count, bank):
+            e, first = divmod(slot, C)
+            sums = psum.tile([P, len(rows), count], F32, name="y_sums", tag=bank)
             for at, j in enumerate(rows):
                 nc.tensor.matmul_mx(
                     out=sums[:, at, :],
                     lhsT=w2[:, e, 2 * j * P : 2 * (j + 1) * P].bitcast(FP4X4),
                     lhsT_scale=w2_plane[:, e * N + j * P : e * N + (j + 1) * P],
-                    rhs=h_codes[e][:].bitcast(FP8X4),
-                    rhs_scale=h_bytes[e][:],
+                    rhs=h_codes[e][:, first : first + count].bitcast(FP8X4),
+                    rhs_scale=h_bytes[e][:, first : first + count],
                     start=True,
                     stop=True,
                 )
-            gated = held.tile([P, len(rows), C], F32, name=f"gated{e}_{rows[0]}", tag=tag, align_bytes=64)
-            if gate_now:
-                weights = gates[:, e * C : (e + 1) * C].unsqueeze(1).to_broadcast([P, len(rows), C])
-                nc.vector.tensor_tensor(gated[:], sums[:], weights, MULT)
-            else:
-                nc.scalar.copy(gated[:], sums[:])
-            return {j: gated[:, at, :] for at, j in enumerate(rows)}
+            return sums
 
-        def scatter_on_scalar(j, e, values):
-            nc.scalar.activation(results[j][:].indirect(entries_of(e)), values[j], COPY)
+        def gated_rows(rows, slot, count, bank):
+            sums = y_sums(rows, slot, count, bank)
+            values = held.tile([P, len(rows), count], F32, name=f"gated{slot}_{rows[0]}", align_bytes=64)
+            weights = gates[:, slot : slot + count].unsqueeze(1).to_broadcast([P, len(rows), count])
+            nc.vector.tensor_tensor(values[:], sums[:], weights, MULT)
+            return [values[:, at, :] for at in range(len(rows))]
 
-        def scatter_on_vector(j, e, values):
-            nc.vector.tensor_copy(results[j][:].indirect(entries_of(e)), values[j])
+        def scatter_on_scalar(j, slot, count, values):
+            nc.scalar.activation(windows[j][:].indirect(entries(slot, count)), values, COPY)
 
-        def store(j):
-            queue = nc.scalar if j == ROWS - 1 else nc.sync
-            queue.dma_start(out[j * P : (j + 1) * P, :], results[j][:])
+        def store(j, queue):
+            queue.dma_start(out[j * P : (j + 1) * P, :], windows[j][:])
 
-        nc.vector.tensor_copy(x_codes[0][:, 0:BLOCK], tokens[0][:].indirect(offsets[:, 0 : BLOCK // 16]))
-        nc.vector.tensor_copy(x_codes[0][:, BLOCK:SLOTS], tokens[0][:].indirect(offsets[:, BLOCK // 16 : SLOTS // 16]))
-        unread = psum.tile([P, C], F32, name="unread", tag="bank6")
-        first_bytes = x_codes[0][:, 0:BLOCK].bitcast(U8)
+        gather_words(0)
+        unread = psum.tile([P, H], F32, name="unread", tag="bank6")
+        first_bytes = x_codes[0][:, 0:C].bitcast(U8)
         for repeat in range(WARM_UP):
             nc.tensor.matmul_mx(
                 out=unread[:],
                 lhsT=x_codes[0][:, 0:BLOCK].bitcast(FP8X4),
-                lhsT_scale=first_bytes[:, 0:P],
+                lhsT_scale=first_bytes[:, 0:BLOCK],
                 rhs=first_bytes.bitcast(FP4X4),
-                rhs_scale=first_bytes[:, 0:C],
+                rhs_scale=first_bytes[:, 0:H],
                 start=True,
                 stop=True,
             )
-        load_late()
         for o in range(PASSES):
-            gather_bytes(o, 0, 2, byte_tile(2, f"x_bytes{o}")[:])
-        for e in range(E):
-            nc.vector.tensor_copy(x_codes[1][:, e * C : (e + 1) * C], tokens[1][:].indirect(entries_of(e)))
-        behind_words = byte_tile(3, "tokens1")
-        gather_bytes(0, 2, 2, behind_words[:, 0:C])
+            gather_bytes(o, 0, HALVES, byte_tile(HALVES, f"x_bytes{o}")[:])
+        gather_words(1)
+        behind_words = byte_tile(HALVES + 1, "tokens1")
+        gather_bytes(0, 2, HALVES, behind_words[:, 0:C])
         gather_bytes(1, 2, 1, behind_words[:, C : C + BLOCK])
 
         hidden = [hidden_values(block, a) for block, a in enumerate(gate_sums((0, 1)))]
@@ -229,23 +225,26 @@ def tile_moe_pkd_glu_gelu_kernel(
         hidden.append(hidden_values(2, gate_sums((2,))[0]))
         turn(0, hidden[0])
         turn(1, hidden[1])
-        quantise(0, 0, C)
+        quantise(0)
         hidden.append(hidden_values(3, gate_sums((3,))[0]))
         turn(2, hidden[2])
-        first = second_layer(0, (1,), "bank0", "gated_a")
-        plain = second_layer(0, (0,), "bank6", "plain", False)
-        scatter_on_scalar(1, 0, first)
-        first = {**first, **second_layer(0, (2,), "bank4", "gated_b")}
-        scatter_on_scalar(2, 0, first)
+
+        opening = gated_rows((1,), 0, BLOCK, "bank0")
+        ungated = held.tile([P, 1, C], F32, name="ungated", align_bytes=64)
+        nc.scalar.copy(ungated[:], y_sums((0,), 0, C, "bank6")[:])
+        opening = opening + gated_rows((1,), BLOCK, BLOCK, "bank0")
+        for half in range(HALVES):
+            scatter_on_scalar(1, half * BLOCK, BLOCK, opening[half])
+        scatter_on_scalar(2, 0, C, gated_rows((2,), 0, C, "bank4")[0])
         turn(3, hidden[3])
-        quantise(1, 0, C)
-        first = {**first, **second_layer(0, (3,), "bank1", "gated_f")}
-        scatter_on_scalar(3, 0, first)
-        nc.vector.tensor_tensor(results[0][:].indirect(entries_of(0)), plain[0], gates[:, 0:C], MULT)
-        second = second_layer(1, (0, 1), "bank3", "gated_d")
-        second = {**second, **second_layer(1, (2, 3), "bank2", "gated_c")}
+        quantise(1)
+        scatter_on_scalar(3, 0, C, gated_rows((3,), 0, C, "bank1")[0])
+        nc.vector.tensor_tensor(windows[0][:].indirect(entries(0, C)), ungated[:, 0, :], gates[:, 0:C], MULT)
+
+        for_vector = gated_rows((0, 1), C, C, "bank3")
+        for_scalar = gated_rows((2, 3), C, C, "bank2")
         for j in range(2):
-            scatter_on_scalar(2 + j, 1, second)
-            store(2 + j)
-            scatter_on_vector(j, 1, second)
-            store(j)
+            scatter_on_scalar(2 + j, C, C, for_scalar[j])
+            store(2 + j, nc.scalar if 2 + j == ROWS - 1 else nc.sync)
+            nc.vector.tensor_copy(windows[j][:].indirect(entries(C, C)), for_vector[j])
+            store(j, nc.sync)

@@ -53,9 +53,9 @@ def tile_moe_pkd_glu_gelu_kernel(
         offsets = held.tile([P, SLOTS // PER_COLUMN], U16, name="offsets")
 
         x_plane = held.tile([P, PASSES * T], U8, name="x_plane", align_bytes=64)
-        w1_plane = held.tile([P, E * PASSES * H], U8, name="w1_plane", align_bytes=64)
-        w3_plane = held.tile([P, E * PASSES * H], U8, name="w3_plane", align_bytes=64)
-        w2_plane = held.tile([P, E * N], U8, name="w2_plane", align_bytes=64)
+        w1_plane = held.tile([P, 128 + E * PASSES * H], U8, name="w1_plane", align_bytes=256)[:, 128:]
+        w3_plane = held.tile([P, 128 + E * PASSES * H], U8, name="w3_plane", align_bytes=256)[:, 128:]
+        w2_plane = held.tile([P, 128 + E * N], U8, name="w2_plane", align_bytes=256)[:, 128:]
         nc.gpsimd.memset(x_plane[:].bitcast(I32), 0)
         for plane in (w1_plane, w3_plane):
             nc.vector.memset(plane[:].bitcast(I32), 0)
@@ -64,12 +64,12 @@ def tile_moe_pkd_glu_gelu_kernel(
         nc.gpsimd.memset(w2_plane[:].bitcast(I32), 0)
 
         def load_tokens(o):
-            table = held.tile([P, T], U32, name=f"tokens{o}", tag=f"tokens{o}", align_bytes=64)
+            table = held.tile([P, T], U32, name=f"tokens{o}", tag=f"tokens{o}", align_bytes=256)
             nc.sync.dma_start(table[:].bitcast(I32), x_words[o].rearrange("p t r -> p (t r)").bitcast(I32))
             return table
 
         def load_words(words, e, name):
-            codes = held.tile([P, PASSES, 2 * H], U8, name=name, align_bytes=64)
+            codes = held.tile([P, PASSES, 2 * H], U8, name=name, align_bytes=256)
             nc.sync.dma_start(codes[:].bitcast(I32), words[e].bitcast(I32).rearrange("s p w -> p s w"))
             return codes
 
@@ -84,7 +84,7 @@ def tile_moe_pkd_glu_gelu_kernel(
         w1.append(load_words(w1_words, 1, "w1_1"))
         w3.append(load_words(w3_words, 1, "w3_1"))
         load_scale_rows(nc, w2_plane, w2_scales.rearrange("e s q n -> (e s) q n"), E)
-        w2 = held.tile([P, E, 2 * N], U8, name="w2", align_bytes=64)
+        w2 = held.tile([P, E, 2 * N], U8, name="w2", align_bytes=256)
         nc.sync.dma_start(w2[:].bitcast(I32), w2_words.bitcast(I32).rearrange("e s p w -> p (e s) w"))
         gates = held.tile([P, SLOTS], F32, name="gates")
         nc.sync.dma_start(gates[:], gate[0:P, :])
@@ -100,7 +100,7 @@ def tile_moe_pkd_glu_gelu_kernel(
         def entries(slot, count):
             return offsets[:, slot // PER_COLUMN : (slot + count) // PER_COLUMN]
 
-        x_codes = [held.tile([P, SLOTS], U32, name=f"x_codes{o}", align_bytes=64) for o in range(PASSES)]
+        x_codes = [held.tile([P, 16 + SLOTS], U32, name=f"x_codes{o}", align_bytes=256)[:, 16:] for o in range(PASSES)]
         x_bytes = {}
 
         def gather_words(o):
@@ -108,7 +108,7 @@ def tile_moe_pkd_glu_gelu_kernel(
                 nc.vector.tensor_copy(x_codes[o][:, e * C : (e + 1) * C], tokens[o][:].indirect(entries(e * C, C)))
 
         def byte_tile(blocks, tag):
-            return held.tile([P, blocks * BLOCK], U8, name=f"bytes_{tag}", tag=tag, align_bytes=64)
+            return held.tile([P, 192 + blocks * BLOCK], U8, name=f"bytes_{tag}", tag=tag, align_bytes=256)[:, 192:]
 
         def gather_bytes(o, first_block, blocks, target):
             picked = entries(first_block * BLOCK, blocks * BLOCK)
@@ -141,7 +141,7 @@ def tile_moe_pkd_glu_gelu_kernel(
 
         def hidden_values(block, a):
             parts = (slice(0, 1), slice(1, 2)) if block == LAST_BLOCK else (slice(0, 2),)
-            act = held.tile([P, 2, P, 2], F32, name=f"act{block}", tag=f"act{block}", align_bytes=64)
+            act = held.tile([P, 2, P, 2], F32, name=f"act{block}", tag=f"act{block}", align_bytes=256)
             for part in parts:
                 nc.scalar.activation(act[:, part], by_pairs(a)[:, part], GELU)
             b = psum.tile([P, H], F32, name=f"b{block}", tag=UP_BANKS[block])
@@ -166,8 +166,8 @@ def tile_moe_pkd_glu_gelu_kernel(
                 turned[:].rearrange("p u r -> p r u"),
             )
 
-        h_codes = [held.tile([P, C], U32, name=f"h_codes{e}", align_bytes=64) for e in range(E)]
-        h_bytes = [held.tile([P, C], U8, name=f"h_bytes{e}", align_bytes=64) for e in range(E)]
+        h_codes = [held.tile([P, 16 + C], U32, name=f"h_codes{e}", align_bytes=256)[:, 16:] for e in range(E)]
+        h_bytes = [held.tile([P, 192 + C], U8, name=f"h_bytes{e}", align_bytes=256)[:, 192:] for e in range(E)]
 
         def quantise(e):
             nc.vector.quantize_mx(out=h_codes[e][:].bitcast(FP8X4), scales=h_bytes[e][:], in_=grouped[e][:])

@@ -26,6 +26,7 @@ LAST_BLOCK = SLOTS // BLOCK - 1
 HALVES = C // BLOCK
 ROWS = N // P
 PER_COLUMN = 16
+HANDED = 32
 WARM_UP = 2
 
 GATE_BANKS = ("bank0", "bank2", "bank4", "bank3")
@@ -187,9 +188,10 @@ def tile_moe_pkd_glu_gelu_kernel(
                 )
             return sums
 
-        def gated_rows(rows, slot, count, bank):
+        def gated_rows(rows, slot, count, bank, values=None):
             sums = y_sums(rows, slot, count, bank)
-            values = held.tile([P, len(rows), count], F32, name=f"gated{slot}_{rows[0]}", align_bytes=64)
+            if values is None:
+                values = held.tile([P, len(rows), count], F32, name=f"gated{slot}_{rows[0]}", align_bytes=64)
             weights = gates[:, slot : slot + count].unsqueeze(1).to_broadcast([P, len(rows), count])
             nc.vector.tensor_tensor(values[:], sums[:], weights, MULT)
             return [values[:, at, :] for at in range(len(rows))]
@@ -232,19 +234,22 @@ def tile_moe_pkd_glu_gelu_kernel(
         opening = gated_rows((1,), 0, BLOCK, "bank0")
         ungated = held.tile([P, 1, C], F32, name="ungated", align_bytes=64)
         nc.scalar.copy(ungated[:], y_sums((0,), 0, C, "bank6")[:])
-        opening = opening + gated_rows((1,), BLOCK, BLOCK, "bank0")
-        for half in range(HALVES):
-            scatter_on_scalar(1, half * BLOCK, BLOCK, opening[half])
+        late = held.tile([P, BLOCK + 2 * C], F32, name="late", align_bytes=64)
+        gated_rows((1,), BLOCK, BLOCK, "bank0", late[:, 0:BLOCK].unsqueeze(1))
+        scatter_on_scalar(1, 0, BLOCK, opening[0])
+        scatter_on_scalar(1, BLOCK, BLOCK - HANDED, late[:, 0 : BLOCK - HANDED])
         scatter_on_scalar(2, 0, C, gated_rows((2,), 0, C, "bank4")[0])
         turn(3, hidden[3])
         quantise(1)
         scatter_on_scalar(3, 0, C, gated_rows((3,), 0, C, "bank1")[0])
         nc.vector.tensor_tensor(windows[0][:].indirect(entries(0, C)), ungated[:, 0, :], gates[:, 0:C], MULT)
 
-        for_vector = gated_rows((0, 1), C, C, "bank3")
+        gated_rows((1, 0), C, C, "bank3", late[:, BLOCK:].rearrange("p (r c) -> p r c", r=2))
+        for_vector = ((C, late[:, BLOCK + C :]), (C - HANDED, late[:, BLOCK - HANDED : BLOCK + C]))
         for_scalar = gated_rows((2, 3), C, C, "bank2")
         for j in range(2):
             scatter_on_scalar(2 + j, C, C, for_scalar[j])
             store(2 + j, nc.scalar if 2 + j == ROWS - 1 else nc.sync)
-            nc.vector.tensor_copy(windows[j][:].indirect(entries(C, C)), for_vector[j])
+            slot, values = for_vector[j]
+            nc.vector.tensor_copy(windows[j][:].indirect(entries(slot, SLOTS - slot)), values)
             store(j, nc.sync)

@@ -248,8 +248,8 @@ def tile_moe_pkd_glu_gelu_kernel(
         for_vector = ((C, late[:, BLOCK + C :]), (C - HANDED, late[:, BLOCK - HANDED : BLOCK + C]))
         for_scalar = gated_rows((2, 3), C, C, "bank2")
         for j in range(2):
-            scatter_on_scalar(2 + j, C, C, for_scalar[j])
-            store(2 + j, nc.scalar if 2 + j == ROWS - 1 else nc.sync)
             slot, values = for_vector[j]
             nc.vector.tensor_copy(windows[j][:].indirect(entries(slot, SLOTS - slot)), values)
             store(j, nc.sync)
+            scatter_on_scalar(2 + j, C, C, for_scalar[j])
+            store(2 + j, nc.sync)

@@ -64,20 +64,22 @@ def tile_moe_pkd_glu_gelu_kernel(
         make_identity(nc, identity[:])
         nc.gpsimd.memset(w2_plane[:].bitcast(I32), 0)
 
+        tokens = held.tile([P, PASSES * T], U32, name="tokens", tag="tokens", align_bytes=256)
+
         def load_tokens(o):
-            table = held.tile([P, T], U32, name=f"tokens{o}", tag=f"tokens{o}", align_bytes=256)
-            nc.sync.dma_start(table[:].bitcast(I32), x_words[o].rearrange("p t r -> p (t r)").bitcast(I32))
-            return table
+            nc.sync.dma_start(
+                tokens[:, o * T : (o + 1) * T].bitcast(I32), x_words[o].rearrange("p t r -> p (t r)").bitcast(I32)
+            )
 
         def load_words(words, e, name):
             codes = held.tile([P, PASSES, 2 * H], U8, name=name, align_bytes=256)
             nc.sync.dma_start(codes[:].bitcast(I32), words[e].bitcast(I32).rearrange("s p w -> p s w"))
             return codes
 
-        tokens = [load_tokens(0)]
+        load_tokens(0)
         nc.sync.dma_start(offsets[:], offs)
         load_scale_rows(nc, x_plane, x_scales, PASSES)
-        tokens.append(load_tokens(1))
+        load_tokens(1)
         w1 = [load_words(w1_words, 0, "w1_0")]
         load_scale_rows(nc, w1_plane, w1_scales.rearrange("e s q i -> (e s) q i"), E * PASSES)
         w3 = [load_words(w3_words, 0, "w3_0")]
@@ -104,9 +106,9 @@ def tile_moe_pkd_glu_gelu_kernel(
         x_codes = [held.tile([P, 16 + SLOTS], U32, name=f"x_codes{o}", align_bytes=256)[:, 16:] for o in range(PASSES)]
         x_bytes = {}
 
-        def gather_words(o):
-            for e in range(E):
-                nc.vector.tensor_copy(x_codes[o][:, e * C : (e + 1) * C], tokens[o][:].indirect(entries(e * C, C)))
+        def gather_words(o, e, spare=0):
+            window = tokens[:, o * T : (o + 1) * T + spare]
+            nc.vector.tensor_copy(x_codes[o][:, e * C : (e + 1) * C], window.indirect(entries(e * C, C)))
 
         def byte_tile(blocks, tag):
             return held.tile([P, 192 + blocks * BLOCK], U8, name=f"bytes_{tag}", tag=tag, align_bytes=256)[:, 192:]
@@ -202,7 +204,7 @@ def tile_moe_pkd_glu_gelu_kernel(
         def store(j, queue):
             queue.dma_start(out[j * P : (j + 1) * P, :], windows[j][:])
 
-        gather_words(0)
+        gather_words(0, 0)
         unread = psum.tile([P, H], F32, name="unread", tag="bank6")
         first_bytes = x_codes[0][:, 0:C].bitcast(U8)
         for repeat in range(WARM_UP):
@@ -217,13 +219,17 @@ def tile_moe_pkd_glu_gelu_kernel(
             )
         for o in range(PASSES):
             gather_bytes(o, 0, HALVES, byte_tile(HALVES, f"x_bytes{o}")[:])
-        gather_words(1)
-        behind_words = byte_tile(HALVES + 1, "tokens1")
-        gather_bytes(0, 2, HALVES, behind_words[:, 0:C])
-        gather_bytes(1, 2, 1, behind_words[:, C : C + BLOCK])
+        gather_words(1, 0)
+        gather_words(0, 1, spare=8)
+        gather_words(1, 1)
+        behind_words = byte_tile(PASSES, "tokens")
+        for o in range(PASSES):
+            gather_bytes(o, 2, 1, behind_words[:, o * BLOCK : (o + 1) * BLOCK])
 
         hidden = [hidden_values(block, a) for block, a in enumerate(gate_sums((0, 1)))]
-        gather_bytes(1, 3, 1, byte_tile(1, "act1")[:])
+        behind_products = byte_tile(PASSES, "act0")
+        for o in range(PASSES):
+            gather_bytes(o, 3, 1, behind_products[:, o * BLOCK : (o + 1) * BLOCK])
         hidden.append(hidden_values(2, gate_sums((2,))[0]))
         turn(0, hidden[0])
         turn(1, hidden[1])

@@ -27,7 +27,7 @@ HALVES = C // BLOCK
 ROWS = N // P
 PER_COLUMN = 16
 HANDED = 32
-WARM_UP = 2
+WARM_UP = 4
 
 GATE_BANKS = ("bank0", "bank2", "bank4", "bank3")
 UP_BANKS = ("bank1", "bank3", "bank5", "bank2")
@@ -106,9 +106,9 @@ def tile_moe_pkd_glu_gelu_kernel(
         x_codes = [held.tile([P, 16 + SLOTS], U32, name=f"x_codes{o}", align_bytes=256)[:, 16:] for o in range(PASSES)]
         x_bytes = {}
 
-        def gather_words(o, e, spare=0):
+        def gather_words(o, slot, count, spare=0):
             window = tokens[:, o * T : (o + 1) * T + spare]
-            nc.vector.tensor_copy(x_codes[o][:, e * C : (e + 1) * C], window.indirect(entries(e * C, C)))
+            nc.vector.tensor_copy(x_codes[o][:, slot : slot + count], window.indirect(entries(slot, count)))
 
         def byte_tile(blocks, tag):
             return held.tile([P, 192 + blocks * BLOCK], U8, name=f"bytes_{tag}", tag=tag, align_bytes=256)[:, 192:]
@@ -204,24 +204,25 @@ def tile_moe_pkd_glu_gelu_kernel(
         def store(j, queue):
             queue.dma_start(out[j * P : (j + 1) * P, :], windows[j][:])
 
-        gather_words(0, 0)
-        unread = psum.tile([P, H], F32, name="unread", tag="bank6")
-        first_bytes = x_codes[0][:, 0:C].bitcast(U8)
+        gather_words(0, 0, BLOCK)
+        unread = psum.tile([P, C], F32, name="unread", tag="bank6")
+        first_bytes = x_codes[0][:, 0:BLOCK].bitcast(U8)
         for repeat in range(WARM_UP):
             nc.tensor.matmul_mx(
                 out=unread[:],
                 lhsT=x_codes[0][:, 0:BLOCK].bitcast(FP8X4),
                 lhsT_scale=first_bytes[:, 0:BLOCK],
                 rhs=first_bytes.bitcast(FP4X4),
-                rhs_scale=first_bytes[:, 0:H],
+                rhs_scale=first_bytes[:, 0:C],
                 start=True,
                 stop=True,
             )
+        gather_words(0, BLOCK, BLOCK)
         for o in range(PASSES):
             gather_bytes(o, 0, HALVES, byte_tile(HALVES, f"x_bytes{o}")[:])
-        gather_words(1, 0)
-        gather_words(0, 1, spare=8)
-        gather_words(1, 1)
+        gather_words(1, 0, C)
+        gather_words(0, C, C, spare=8)
+        gather_words(1, C, C)
         behind_words = byte_tile(PASSES, "tokens")
         for o in range(PASSES):
             gather_bytes(o, 2, 1, behind_words[:, o * BLOCK : (o + 1) * BLOCK])

from contextlib import ExitStack

import concourse.mybir as mybir
from concourse.masks import make_identity

K, T, E, C, H, N = 1024, 640, 2, 256, 512, 512
SLOTS = E * C
FLOPS = 2 * SLOTS * (2 * K * H + H * N)

F32 = mybir.dt.float32
BF16 = mybir.dt.bfloat16
I32 = mybir.dt.int32
U32 = mybir.dt.uint32
U16 = mybir.dt.uint16
U8 = mybir.dt.uint8
FP8X4 = mybir.dt.float8_e4m3fn_x4
FP4X4 = mybir.dt.float4_e2m1fn_x4
GELU = mybir.ActivationFunctionType.Gelu_apprx_tanh
COPY = mybir.ActivationFunctionType.Copy
MULT = mybir.AluOpType.mult

P = 128
PASSES = K // 512
BLOCK = 128
LAST_BLOCK = SLOTS // BLOCK - 1
HALVES = C // BLOCK
ROWS = N // P
PER_COLUMN = 16
HANDED = 32
WARM_UP = 4

GATE_BANKS = ("bank0", "bank2", "bank4", "bank3")
UP_BANKS = ("bank1", "bank3", "bank5", "bank2")
TURN_BANKS = ("bank6", "bank1", "bank7", "bank5")


def load_scale_rows(nc, plane, rows, groups):
    words = rows.bitcast(I32)
    for r in range(4):
        nc.sync.dma_start(
            out=plane[r:P:32, :].bitcast(I32).rearrange("p (g w) -> p g w", g=groups),
            in_=words[:, r:16:4, :].rearrange("g q w -> q g w"),
        )


def tile_moe_pkd_glu_gelu_kernel(
    tc, x_words, x_scales, w1_words, w1_scales, w3_words, w3_scales, w2_words, w2_scales, gate, offs, out
):
    nc = tc.nc
    with ExitStack() as ctx:
        held = ctx.enter_context(tc.tile_pool(name="held", bufs=1))
        psum = ctx.enter_context(tc.psum_pool(name="psum", bufs=1))

        offsets = held.tile([P, SLOTS // PER_COLUMN], U16, name="offsets")

        x_plane = held.tile([P, PASSES * T], U8, name="x_plane", align_bytes=64)
        w1_plane = held.tile([P, 128 + E * PASSES * H], U8, name="w1_plane", align_bytes=256)[:, 128:]
        w3_plane = held.tile([P, 128 + E * PASSES * H], U8, name="w3_plane", align_bytes=256)[:, 128:]
        w2_plane = held.tile([P, 128 + E * N], U8, name="w2_plane", align_bytes=256)[:, 128:]
        nc.gpsimd.memset(x_plane[:].bitcast(I32), 0)
        for plane in (w1_plane, w3_plane):
            nc.vector.memset(plane[:].bitcast(I32), 0)
        identity = held.tile([P, P], F32, name="identity")
        make_identity(nc, identity[:])
        nc.gpsimd.memset(w2_plane[:].bitcast(I32), 0)

        tokens = held.tile([P, PASSES * T], U32, name="tokens", tag="tokens", align_bytes=256)

        def load_tokens(o):
            nc.sync.dma_start(
                tokens[:, o * T : (o + 1) * T].bitcast(I32), x_words[o].rearrange("p t r -> p (t r)").bitcast(I32)
            )

        def load_words(words, e, name):
            codes = held.tile([P, PASSES, 2 * H], U8, name=name, align_bytes=256)
            nc.sync.dma_start(codes[:].bitcast(I32), words[e].bitcast(I32).rearrange("s p w -> p s w"))
            return codes

        load_tokens(0)
        nc.sync.dma_start(offsets[:], offs)
        load_scale_rows(nc, x_plane, x_scales, PASSES)
        load_tokens(1)
        w1 = [load_words(w1_words, 0, "w1_0")]
        load_scale_rows(nc, w1_plane, w1_scales.rearrange("e s q i -> (e s) q i"), E * PASSES)
        w3 = [load_words(w3_words, 0, "w3_0")]
        load_scale_rows(nc, w3_plane, w3_scales.rearrange("e s q i -> (e s) q i"), E * PASSES)
        w1.append(load_words(w1_words, 1, "w1_1"))
        w3.append(load_words(w3_words, 1, "w3_1"))
        load_scale_rows(nc, w2_plane, w2_scales.rearrange("e s q n -> (e s) q n"), E)
        w2 = held.tile([P, E, 2 * N], U8, name="w2", align_bytes=256)
        nc.sync.dma_start(w2[:].bitcast(I32), w2_words.bitcast(I32).rearrange("e s p w -> p (e s) w"))
        gates = held.tile([P, SLOTS], F32, name="gates")
        nc.sync.dma_start(gates[:], gate[0:P, :])

        zero = held.tile([P, 1], F32, name="zero")
        nc.vector.memset(zero[:], 0.0)
        windows = []
        for j in range(ROWS):
            window = held.tile([P, T], F32, name=f"window{j}")
            nc.scalar.activation(window[:], zero[:].to_broadcast([P, T]), GELU)
            windows.append(window)

        def entries(slot, count):
            return offsets[:, slot // PER_COLUMN : (slot + count) // PER_COLUMN]

        x_codes = [held.tile([P, 16 + SLOTS], U32, name=f"x_codes{o}", align_bytes=256)[:, 16:] for o in range(PASSES)]
        x_bytes = {}

        def gather_words(o, slot, count, spare=0):
            window = tokens[:, o * T : (o + 1) * T + spare]
            nc.vector.tensor_copy(x_codes[o][:, slot : slot + count], window.indirect(entries(slot, count)))

        def byte_tile(blocks, tag):
            return held.tile([P, 192 + blocks * BLOCK], U8, name=f"bytes_{tag}", tag=tag, align_bytes=256)[:, 192:]

        def gather_bytes(o, first_block, blocks, target):
            picked = entries(first_block * BLOCK, blocks * BLOCK)
            nc.vector.tensor_copy(target, x_plane[:, o * T : (o + 1) * T].indirect(picked))
            for b in range(blocks):
                x_bytes.setdefault((first_block + b, o), target[:, b * BLOCK : (b + 1) * BLOCK])

        def multiply(sums, block, o, words, plane):
            e = block // HALVES
            at = (e * PASSES + o) * H
            nc.tensor.matmul_mx(
                out=sums[:],
                lhsT=x_codes[o][:, block * BLOCK : (block + 1) * BLOCK].bitcast(FP8X4),
                lhsT_scale=x_bytes[(block, o)],
                rhs=words[e][:, o, :].bitcast(FP4X4),
                rhs_scale=plane[:, at : at + H],
                start=(o == 0),
                stop=(o == PASSES - 1),
            )

        def gate_sums(blocks):
            banks = [psum.tile([P, H], F32, name=f"a{block}", tag=GATE_BANKS[block]) for block in blocks]
            for o in range(PASSES):
                for block, sums in zip(blocks, banks):
                    multiply(sums, block, o, w1, w1_plane)
            return banks

        def by_pairs(bank):
            return bank[:].rearrange("p (q u v) -> p u q v", u=2, v=2)

        def hidden_values(block, a):
            parts = (slice(0, 1), slice(1, 2)) if block == LAST_BLOCK else (slice(0, 2),)
            act = held.tile([P, 2, P, 2], F32, name=f"act{block}", tag=f"act{block}", align_bytes=256)
            for part in parts:
                nc.scalar.activation(act[:, part], by_pairs(a)[:, part], GELU)
            b = psum.tile([P, H], F32, name=f"b{block}", tag=UP_BANKS[block])
            for o in range(PASSES):
                multiply(b, block, o, w3, w3_plane)
            product = held.tile([P, 2, P, 2], BF16, name=f"hidden{block}", align_bytes=64)
            for part in parts:
                nc.vector.tensor_tensor(product[:, part], by_pairs(b)[:, part], act[:, part], MULT)
            return product

        grouped = [held.tile([P, 4 * C], BF16, name=f"grouped{e}", align_bytes=64) for e in range(E)]

        def turn(block, values):
            e, half = divmod(block, HALVES)
            pairs = values[:].rearrange("p u q v -> p (u q v)").bitcast(F32)
            turned = psum.tile([P, 2, BLOCK], F32, name=f"turned{block}", tag=TURN_BANKS[block])
            for u in range(2):
                nc.tensor.transpose(turned[:, u, :], pairs[:, u * P : (u + 1) * P], identity[:])
            copy = nc.vector.tensor_copy if block == LAST_BLOCK else nc.scalar.copy
            copy(
                grouped[e][:, 4 * half * BLOCK : 4 * (half + 1) * BLOCK].bitcast(F32).rearrange("p (r u) -> p r u", u=2),
                turned[:].rearrange("p u r -> p r u"),
            )

        h_codes = [held.tile([P, 16 + C], U32, name=f"h_codes{e}", align_bytes=256)[:, 16:] for e in range(E)]
        h_bytes = [held.tile([P, 192 + C], U8, name=f"h_bytes{e}", align_bytes=256)[:, 192:] for e in range(E)]

        def quantise(e):
            nc.vector.quantize_mx(out=h_codes[e][:].bitcast(FP8X4), scales=h_bytes[e][:], in_=grouped[e][:])

        def y_sums(rows, slot, count, bank):
            e, first = divmod(slot, C)
            sums = psum.tile([P, len(rows), count], F32, name="y_sums", tag=bank)
            for at, j in enumerate(rows):
                nc.tensor.matmul_mx(
                    out=sums[:, at, :],
                    lhsT=w2[:, e, 2 * j * P : 2 * (j + 1) * P].bitcast(FP4X4),
                    lhsT_scale=w2_plane[:, e * N + j * P : e * N + (j + 1) * P],
                    rhs=h_codes[e][:, first : first + count].bitcast(FP8X4),
                    rhs_scale=h_bytes[e][:, first : first + count],
                    start=True,
                    stop=True,
                )
            return sums

        def gated_rows(rows, slot, count, bank, values=None):
            sums = y_sums(rows, slot, count, bank)
            if values is None:
                values = held.tile([P, len(rows), count], F32, name=f"gated{slot}_{rows[0]}", align_bytes=64)
            weights = gates[:, slot : slot + count].unsqueeze(1).to_broadcast([P, len(rows), count])
            nc.vector.tensor_tensor(values[:], sums[:], weights, MULT)
            return [values[:, at, :] for at in range(len(rows))]

        def scatter_on_scalar(j, slot, count, values):
            nc.scalar.activation(windows[j][:].indirect(entries(slot, count)), values, COPY)

        def store(j, queue):
            queue.dma_start(out[j * P : (j + 1) * P, :], windows[j][:])

        gather_words(0, 0, BLOCK)
        unread = psum.tile([P, C], F32, name="unread", tag="bank6")
        first_bytes = x_codes[0][:, 0:BLOCK].bitcast(U8)
        for repeat in range(WARM_UP):
            nc.tensor.matmul_mx(
                out=unread[:],
                lhsT=x_codes[0][:, 0:BLOCK].bitcast(FP8X4),
                lhsT_scale=first_bytes[:, 0:BLOCK],
                rhs=first_bytes.bitcast(FP4X4),
                rhs_scale=first_bytes[:, 0:C],
                start=True,
                stop=True,
            )
        gather_words(0, BLOCK, BLOCK)
        for o in range(PASSES):
            gather_bytes(o, 0, HALVES, byte_tile(HALVES, f"x_bytes{o}")[:])
        gather_words(1, 0, C)
        gather_words(0, C, C, spare=8)
        gather_words(1, C, C)
        behind_words = byte_tile(PASSES, "tokens")
        for o in range(PASSES):
            gather_bytes(o, 2, 1, behind_words[:, o * BLOCK : (o + 1) * BLOCK])

        hidden = [hidden_values(block, a) for block, a in enumerate(gate_sums((0, 1)))]
        behind_products = byte_tile(PASSES, "act0")
        for o in range(PASSES):
            gather_bytes(o, 3, 1, behind_products[:, o * BLOCK : (o + 1) * BLOCK])
        hidden.append(hidden_values(2, gate_sums((2,))[0]))
        turn(0, hidden[0])
        turn(1, hidden[1])
        quantise(0)
        hidden.append(hidden_values(3, gate_sums((3,))[0]))
        turn(2, hidden[2])

        opening = gated_rows((1,), 0, BLOCK, "bank0")
        ungated = held.tile([P, 1, C], F32, name="ungated", align_bytes=64)
        nc.scalar.copy(ungated[:], y_sums((0,), 0, C, "bank6")[:])
        late = held.tile([P, BLOCK + 2 * C], F32, name="late", align_bytes=64)
        gated_rows((1,), BLOCK, BLOCK, "bank0", late[:, 0:BLOCK].unsqueeze(1))
        scatter_on_scalar(1, 0, BLOCK, opening[0])
        scatter_on_scalar(1, BLOCK, BLOCK - HANDED, late[:, 0 : BLOCK - HANDED])
        scatter_on_scalar(2, 0, C, gated_rows((2,), 0, C, "bank4")[0])
        turn(3, hidden[3])
        quantise(1)
        scatter_on_scalar(3, 0, C, gated_rows((3,), 0, C, "bank1")[0])
        nc.vector.tensor_tensor(windows[0][:].indirect(entries(0, C)), ungated[:, 0, :], gates[:, 0:C], MULT)

        gated_rows((1, 0), C, C, "bank3", late[:, BLOCK:].rearrange("p (r c) -> p r c", r=2))
        for_vector = ((C, late[:, BLOCK + C :]), (C - HANDED, late[:, BLOCK - HANDED : BLOCK + C]))
        for_scalar = gated_rows((2, 3), C, C, "bank2")
        for j in range(2):
            slot, values = for_vector[j]
            nc.vector.tensor_copy(windows[j][:].indirect(entries(slot, SLOTS - slot)), values)
            store(j, nc.sync)
            scatter_on_scalar(2 + j, C, C, for_scalar[j])
            store(2 + j, nc.sync)
